import numpy as np
import ml_dtypes


def mxq(x, axis, fmt="e4m3"):
    dtype, down = {"e4m3": (ml_dtypes.float8_e4m3fn, 7), "e5m2": (ml_dtypes.float8_e5m2, 14)}[fmt]
    v = np.moveaxis(np.asarray(x, np.float32).astype(ml_dtypes.bfloat16).astype(np.float64), axis, -1)
    blocks = v.reshape(v.shape[:-1] + (-1, 32))
    amax = np.abs(blocks).max(-1, keepdims=True)
    byte = np.maximum(np.where(amax > 0, np.frexp(amax)[1] - 1 + 127, 0) - down, 1)
    scale = np.exp2(byte - 127.0)
    codes = (blocks / scale).astype(np.float32).astype(dtype).astype(np.float64)
    return np.moveaxis((codes * scale).reshape(v.shape), -1, axis)


WIDE = False


def mx_kscale(k):
    if not WIDE:
        return np.ones(k)
    levels = np.array([18, -18])
    if k % 512:
        return np.exp2(np.random.permutation(np.resize(levels, k // 32))).repeat(32)
    a = np.empty((k // 512, 16))
    for p in range(k // 512):
        a[p, :8] = np.random.permutation(np.resize(levels, 8))
        for g in range(8):
            far = levels[np.abs(levels - a[p, g]) >= 10]
            a[p, g + 8] = far[np.random.randint(len(far))]
    return np.exp2(a.ravel()).repeat(32)


def f64(x):
    return np.asarray(x).astype(np.float64)


def striped(idx):
    return np.tile(np.asarray(idx).reshape(-1, 16).T, (8, 1)).astype(np.uint16)


def unstriped(offs):
    return offs[:16].T.reshape(-1).astype(np.int64)


B, N, T, D, R = 1, 512, 2048, 512, 1024


def setup_inputs():
    n = np.random.standard_normal
    idx = np.random.permutation(T)[:B * N]
    s = mx_kscale(D)[:, None]
    u = np.ones(T)
    u[idx] = mx_kscale(B * N)
    r = np.random.uniform(0.5, 2.0, T) * u
    x = n((B, D, R))
    return {
        "xT": (x * s).astype(np.float32),
        "wT": (n((D, T)) * (1.00 / np.sqrt(D)) / s / r).astype(np.float32),
        "y": (2 * np.random.randint(0, 2, (B, R, N)) - 1).astype(np.float32),
        "wt": (np.random.uniform(0.5, 1.5, (B, R, 1)) * 1.0 / np.sqrt(R)).astype(np.float32),
        "ts": np.tile(r, (128, 1)).astype(np.float32),
        "offs": striped(idx),
    }


def reference(xT, wT, y, wt, ts, offs):
    idx = unstriped(offs)
    pick = lambda x: x[:, idx].reshape(x.shape[0], B, N).transpose(1, 0, 2)
    w = pick(f64(wT))
    a = mxq(f64(xT), 1, "e4m3").transpose(0, 2, 1) @ mxq(w, 1, "e4m3")
    ts_ = pick(f64(ts))[:, :1, :]
    a = a * ts_
    g = -f64(wt) * f64(y) / (1.0 + np.exp(f64(y) * a))
    g = g * ts_
    gx = mxq(g, 2, "e5m2") @ mxq(w, 2, "e4m3").transpose(0, 2, 1)
    return gx

@@ -1,0 +1,166 @@
+from contextlib import ExitStack
+
+import concourse.mybir as mybir
+from concourse.masks import make_identity
+
+N, T, D, R = 512, 2048, 512, 1024
+FLOPS = 2 * 2 * R * N * D
+
+F32 = mybir.dt.float32
+BF16 = mybir.dt.bfloat16
+U32 = mybir.dt.uint32
+U16 = mybir.dt.uint16
+U8 = mybir.dt.uint8
+E4M3 = mybir.dt.float8_e4m3fn_x4
+E5M2 = mybir.dt.float8_e5m2_x4
+MULT = mybir.AluOpType.mult
+COPY = mybir.ActivationFunctionType.Copy
+SIGMOID = mybir.ActivationFunctionType.Sigmoid
+
+P = 128
+PACK = 4
+TILES = R // P
+PAIR = 2
+
+
+def tile_attend_gsig_x_ts_kernel(tc, xT, wT, y, wt, ts, offs, out):
+    nc = tc.nc
+    with ExitStack() as ctx:
+        keep = ctx.enter_context(tc.tile_pool(name="keep", bufs=1))
+        ring = ctx.enter_context(tc.tile_pool(name="ring", bufs=3))
+        psum = ctx.enter_context(tc.psum_pool(name="psum", bufs=1))
+
+        offsets = keep.tile([P, N // 16], U16, name="offsets")
+        w_rows = wT.rearrange("(p t) c -> p t c", t=PACK)
+        planes = [keep.tile([P, T], F32, name="plane%d" % t) for t in range(PACK)]
+        ts_runs = keep.tile([P, T // P], F32, name="ts_runs")
+        nc.sync.dma_start(ts_runs[:], ts[0].rearrange("(n m) -> n m", n=P))
+        nc.sync.dma_start(planes[0][:], w_rows[:, 0, :])
+        nc.sync.dma_start(offsets[:], offs)
+        for t in range(1, PACK):
+            nc.sync.dma_start(planes[t][:], w_rows[:, t, :])
+
+        x_rows = xT[0].rearrange("(p t) r -> p t r", t=PACK)
+        y_rows = y[0].rearrange("(k p) i -> p k i", p=P)
+        x_raw, y_raw = [], []
+        for c in range(TILES // PAIR):
+            x_raw.append(keep.tile([P, PACK, PAIR * P], F32, name="x_raw%d" % c))
+            y_raw.append(keep.tile([P, PAIR, N], F32, name="y_raw%d" % c))
+            nc.sync.dma_start(x_raw[c][:], x_rows[:, :, c * PAIR * P : (c + 1) * PAIR * P])
+            nc.sync.dma_start(y_raw[c][:], y_rows[:, c * PAIR : (c + 1) * PAIR, :])
+
+        ident = keep.tile([P, P], F32, name="ident")
+        make_identity(nc, ident[:])
+        warm = keep.tile([P, 1], F32, name="warm")
+        nc.scalar.activation(warm[:], ident[:, 0:1], SIGMOID)
+
+        ts_window = keep.tile([P, T], F32, name="ts_window")
+        window_runs = ts_window[:].rearrange("p (n m) -> p n m", n=P)
+        for b in range(T // P // PACK):
+            spread = psum.tile([P, PACK, P], F32, name="spread", tag="scores", bufs=3)
+            for m in range(PACK):
+                column = b * PACK + m
+                nc.tensor.transpose(spread[:, m, :], ts_runs[:, column : column + 1].to_broadcast([P, P]), ident[:])
+            nc.scalar.copy(window_runs[:, :, b * PACK : (b + 1) * PACK], spread[:].rearrange("p m n -> p n m"))
+
+        wt_rows = keep.tile([P, P], F32, name="wt_rows")
+        nc.gpsimd.memset(wt_rows[:], 0.0)
+        nc.scalar.dma_start(wt_rows[0:TILES, :], wt[0].rearrange("(k p) o -> k (p o)", p=P))
+        wt_turned = psum.tile([P, PACK, P], F32, name="wt_turned", tag="turn", bufs=3)
+        nc.tensor.transpose(wt_turned[:, 0, :], wt_rows[:], ident[:])
+        neg_wt = keep.tile([P, TILES], F32, name="neg_wt")
+        nc.scalar.activation(neg_wt[:], wt_turned[:, 0, 0:TILES], COPY, scale=-1.0)
+
+        ts_all = keep.tile([P, N], F32, name="ts_all")
+
+        w_by_d = keep.tile([P, N, PACK], BF16, name="w_by_d", align_bytes=64)
+        w_by_slot = keep.tile([P, P, 2, 2, PACK], BF16, name="w_by_slot", align_bytes=64)
+        w_words = w_by_d[:].rearrange("p i t -> p (i t)").bitcast(F32).rearrange("p (q s u) -> p q s u", s=PACK, u=2)
+        for t in range(PACK):
+            nc.vector.tensor_copy(w_by_d[:, :, t], planes[t][:].indirect(offsets[:]))
+            if t == 1:
+                nc.vector.tensor_copy(ts_all[:], ts_window[:].indirect(offsets[:]))
+            if t % 2 == 1:
+                u = t // 2
+                w_turned = psum.tile([P, PACK, P], F32, name="w_turned", tag="grad", bufs=2)
+                for s in range(PACK):
+                    nc.tensor.transpose(w_turned[:, s, :], w_words[:, :, s, u], ident[:])
+                halves = w_turned[:].rearrange("q s p -> q (s p)").bitcast(BF16)
+                nc.scalar.copy(w_by_slot[:, :, u, :, :], halves.rearrange("q (s p e) -> q p e s", s=PACK, e=2))
+        w1_codes = keep.tile([P, N], U32, name="w1_codes", align_bytes=64)
+        w1_scales = keep.tile([P, N], U8, name="w1_scales", align_bytes=64)
+        nc.vector.quantize_mx(w1_codes[:].bitcast(E4M3), w1_scales[:], w_by_d[:].rearrange("p i t -> p (i t)"))
+        w2_codes = keep.tile([P, D], U32, name="w2_codes", align_bytes=64)
+        w2_scales = keep.tile([P, D], U8, name="w2_scales", align_bytes=64)
+
+        paired = "p (q u e) -> p u q e"
+        scores, signed, sig, h_turned = {}, {}, {}, {}
+
+        def score(k):
+            c, j = divmod(k, PAIR)
+            x_bf = ring.tile([P, P, PACK], BF16, name="x_bf", align_bytes=64)
+            nc.scalar.copy(
+                x_bf[:].rearrange("p (c i) t -> p c t i", i=4),
+                x_raw[c][:, :, j * P : (j + 1) * P].rearrange("p t (c i) -> p c t i", i=4),
+            )
+            x_codes = ring.tile([P, P], U32, name="x_codes", align_bytes=64)
+            x_scales = ring.tile([P, P], U8, name="x_scales", align_bytes=64)
+            nc.vector.quantize_mx(x_codes[:].bitcast(E4M3), x_scales[:], x_bf[:].rearrange("p r t -> p (r t)"))
+            scores[k] = psum.tile([P, N], F32, name="scores", tag="scores", bufs=3)
+            nc.tensor.matmul_mx(
+                scores[k][:], x_codes[:].bitcast(E4M3), x_scales[:], w1_codes[:].bitcast(E4M3), w1_scales[:],
+                start=True, stop=True,
+            )
+            signed[k] = ring.tile([P, 2, P, 2], F32, name="signed", bufs=4)
+            nc.vector.tensor_tensor(
+                signed[k][:], y_raw[c][:, j, :].rearrange(paired, u=2, e=2), ts_all[:].rearrange(paired, u=2, e=2), MULT
+            )
+
+        def logistic(k):
+            margin = ring.tile([P, 2, P, 2], F32, name="margin")
+            nc.vector.tensor_tensor(margin[:], scores[k][:].rearrange(paired, u=2, e=2), signed[k][:], MULT)
+            sig[k] = ring.tile([P, N], F32, name="sig")
+            nc.scalar.activation(sig[k][:], margin[:].rearrange("p u q e -> p (u q e)"), SIGMOID, scale=-1.0)
+
+        def weigh(k):
+            h = ring.tile([P, N], BF16, name="h", align_bytes=64)
+            nc.vector.scalar_tensor_tensor(
+                h[:], sig[k][:], neg_wt[:, k : k + 1], signed[k][:].rearrange("p u q e -> p (u q e)"), MULT, MULT
+            )
+            turned = psum.tile([P, PACK, P], F32, name="h_psum", tag="turn", bufs=3)
+            h_words = h[:].bitcast(F32)
+            for u in range(2):
+                nc.tensor.transpose(turned[:, u, :], h_words[:, u * P : (u + 1) * P], ident[:])
+            h_turned[k] = ring.tile([P, P * PACK], BF16, name="h_turned", align_bytes=64)
+            nc.scalar.copy(
+                h_turned[k][:].bitcast(F32).rearrange("q (r u) -> q r u", u=2),
+                turned[:, 0:2, :].rearrange("q u r -> q r u"),
+            )
+
+        def gradient(k):
+            h_codes = ring.tile([P, P], U32, name="h_codes", align_bytes=64)
+            h_scales = ring.tile([P, P], U8, name="h_scales", align_bytes=64)
+            nc.vector.quantize_mx(h_codes[:].bitcast(E5M2), h_scales[:], h_turned[k][:])
+            grad = psum.tile([P, D], F32, name="grad", tag="grad", bufs=2)
+            nc.tensor.matmul_mx(
+                grad[:], h_codes[:].bitcast(E5M2), h_scales[:], w2_codes[:].bitcast(E4M3), w2_scales[:],
+                start=True, stop=True,
+            )
+            result = ring.tile([P, D], F32, name="result")
+            nc.scalar.copy(result[:], grad[:])
+            nc.sync.dma_start(out[0, k * P : (k + 1) * P, :], result[:])
+
+        score(0)
+        for step in range(TILES + 2):
+            if step + 1 < TILES:
+                score(step + 1)
+            if step < TILES:
+                logistic(step)
+            if step == 0:
+                nc.vector.quantize_mx(
+                    w2_codes[:].bitcast(E4M3), w2_scales[:], w_by_slot[:].rearrange("q p u e s -> q (p u e s)")
+                )
+            if 0 <= step - 1 < TILES:
+                weigh(step - 1)
+            if 0 <= step - 2 < TILES:
+                gradient(step - 2)

@@ -34,7 +34,7 @@ def tile_attend_gsig_x_ts_kernel(tc, xT, wT, y, wt, ts, offs, out):
         w_rows = wT.rearrange("(p t) c -> p t c", t=PACK)
         planes = [keep.tile([P, T], F32, name="plane%d" % t) for t in range(PACK)]
         ts_runs = keep.tile([P, T // P], F32, name="ts_runs")
-        nc.sync.dma_start(ts_runs[:], ts[0].rearrange("(n m) -> n m", n=P))
+        nc.scalar.dma_start(ts_runs[:], ts[0].rearrange("(n m) -> n m", n=P))
         nc.sync.dma_start(planes[0][:], w_rows[:, 0, :])
         nc.sync.dma_start(offsets[:], offs)
         for t in range(1, PACK):
@@ -57,7 +57,7 @@ def tile_attend_gsig_x_ts_kernel(tc, xT, wT, y, wt, ts, offs, out):
         ts_window = keep.tile([P, T], F32, name="ts_window")
         window_runs = ts_window[:].rearrange("p (n m) -> p n m", n=P)
         for b in range(T // P // PACK):
-            spread = psum.tile([P, PACK, P], F32, name="spread", tag="scores", bufs=3)
+            spread = psum.tile([P, PACK, P], F32, name="spread", tag="scores", bufs=4)
             for m in range(PACK):
                 column = b * PACK + m
                 nc.tensor.transpose(spread[:, m, :], ts_runs[:, column : column + 1].to_broadcast([P, P]), ident[:])
@@ -66,101 +66,141 @@ def tile_attend_gsig_x_ts_kernel(tc, xT, wT, y, wt, ts, offs, out):
         wt_rows = keep.tile([P, P], F32, name="wt_rows")
         nc.gpsimd.memset(wt_rows[:], 0.0)
         nc.scalar.dma_start(wt_rows[0:TILES, :], wt[0].rearrange("(k p) o -> k (p o)", p=P))
-        wt_turned = psum.tile([P, PACK, P], F32, name="wt_turned", tag="turn", bufs=3)
+        wt_turned = psum.tile([P, PACK, P], F32, name="wt_turned", tag="turn", bufs=2)
         nc.tensor.transpose(wt_turned[:, 0, :], wt_rows[:], ident[:])
         neg_wt = keep.tile([P, TILES], F32, name="neg_wt")
         nc.scalar.activation(neg_wt[:], wt_turned[:, 0, 0:TILES], COPY, scale=-1.0)
 
         ts_all = keep.tile([P, N], F32, name="ts_all")
+        ts_pair = keep.tile([P, 2, PAIR, P, 2], F32, name="ts_pair")
+        paired = "p (q u e) -> p u q e"
 
         w_by_d = keep.tile([P, N, PACK], BF16, name="w_by_d", align_bytes=64)
         w_by_slot = keep.tile([P, P, 2, 2, PACK], BF16, name="w_by_slot", align_bytes=64)
         w_words = w_by_d[:].rearrange("p i t -> p (i t)").bitcast(F32).rearrange("p (q s u) -> p q s u", s=PACK, u=2)
+
+        def turn_w(u):
+            w_turned = psum.tile([P, PACK, P], F32, name="w_turned", tag="grad", bufs=2)
+            for s in range(PACK):
+                nc.tensor.transpose(w_turned[:, s, :], w_words[:, :, s, u], ident[:])
+            halves = w_turned[:].rearrange("q s p -> q (s p)").bitcast(BF16)
+            nc.scalar.copy(w_by_slot[:, :, u, :, :], halves.rearrange("q (s p e) -> q p e s", s=PACK, e=2))
+
         for t in range(PACK):
             nc.vector.tensor_copy(w_by_d[:, :, t], planes[t][:].indirect(offsets[:]))
             if t == 1:
                 nc.vector.tensor_copy(ts_all[:], ts_window[:].indirect(offsets[:]))
-            if t % 2 == 1:
-                u = t // 2
-                w_turned = psum.tile([P, PACK, P], F32, name="w_turned", tag="grad", bufs=2)
-                for s in range(PACK):
-                    nc.tensor.transpose(w_turned[:, s, :], w_words[:, :, s, u], ident[:])
-                halves = w_turned[:].rearrange("q s p -> q (s p)").bitcast(BF16)
-                nc.scalar.copy(w_by_slot[:, :, u, :, :], halves.rearrange("q (s p e) -> q p e s", s=PACK, e=2))
+                for j in range(PAIR):
+                    nc.scalar.copy(ts_pair[:, :, j, :, :], ts_all[:].rearrange(paired, u=2, e=2))
+                turn_w(0)
         w1_codes = keep.tile([P, N], U32, name="w1_codes", align_bytes=64)
         w1_scales = keep.tile([P, N], U8, name="w1_scales", align_bytes=64)
         nc.vector.quantize_mx(w1_codes[:].bitcast(E4M3), w1_scales[:], w_by_d[:].rearrange("p i t -> p (i t)"))
         w2_codes = keep.tile([P, D], U32, name="w2_codes", align_bytes=64)
         w2_scales = keep.tile([P, D], U8, name="w2_scales", align_bytes=64)
 
-        paired = "p (q u e) -> p u q e"
-        scores, signed, sig, h_turned = {}, {}, {}, {}
+        scores, signed, sig, h_turned, grads = {}, {}, {}, {}, {}
 
-        def score(k):
-            c, j = divmod(k, PAIR)
-            x_bf = ring.tile([P, P, PACK], BF16, name="x_bf", align_bytes=64)
+        def score(c):
+            x_bf = ring.tile([P, PAIR * P, PACK], BF16, name="x_bf", align_bytes=64)
             nc.scalar.copy(
                 x_bf[:].rearrange("p (c i) t -> p c t i", i=4),
-                x_raw[c][:, :, j * P : (j + 1) * P].rearrange("p t (c i) -> p c t i", i=4),
+                x_raw[c][:].rearrange("p t (c i) -> p c t i", i=4),
             )
-            x_codes = ring.tile([P, P], U32, name="x_codes", align_bytes=64)
-            x_scales = ring.tile([P, P], U8, name="x_scales", align_bytes=64)
+            x_codes = ring.tile([P, PAIR * P], U32, name="x_codes", align_bytes=64)
+            x_scales = ring.tile([P, PAIR * P], U8, name="x_scales", align_bytes=64)
             nc.vector.quantize_mx(x_codes[:].bitcast(E4M3), x_scales[:], x_bf[:].rearrange("p r t -> p (r t)"))
-            scores[k] = psum.tile([P, N], F32, name="scores", tag="scores", bufs=3)
-            nc.tensor.matmul_mx(
-                scores[k][:], x_codes[:].bitcast(E4M3), x_scales[:], w1_codes[:].bitcast(E4M3), w1_scales[:],
-                start=True, stop=True,
-            )
-            signed[k] = ring.tile([P, 2, P, 2], F32, name="signed", bufs=4)
-            nc.vector.tensor_tensor(
-                signed[k][:], y_raw[c][:, j, :].rearrange(paired, u=2, e=2), ts_all[:].rearrange(paired, u=2, e=2), MULT
-            )
+            for j in range(PAIR):
+                k = c * PAIR + j
+                rows = slice(j * P, (j + 1) * P)
+                scores[k] = psum.tile([P, N], F32, name="scores", tag="scores", bufs=4)
+                nc.tensor.matmul_mx(
+                    scores[k][:], x_codes[:, rows].bitcast(E4M3), x_scales[:, rows],
+                    w1_codes[:].bitcast(E4M3), w1_scales[:], start=True, stop=True,
+                )
+
+        def sign(c):
+            signed[c] = ring.tile([P, 2, PAIR, P, 2], F32, name="signed", bufs=4)
+            if c == 0:
+                for j in range(PAIR):
+                    nc.vector.tensor_tensor(
+                        signed[c][:, :, j, :, :], y_raw[c][:, j, :].rearrange(paired, u=2, e=2), ts_pair[:, :, j, :, :], MULT
+                    )
+            else:
+                nc.vector.tensor_tensor(
+                    signed[c][:].rearrange("p u j q e -> p u (j q) e"),
+                    y_raw[c][:].rearrange("p j (q u e) -> p u (j q) e", u=2, e=2),
+                    ts_pair[:].rearrange("p u j q e -> p u (j q) e"),
+                    MULT,
+                )
 
         def logistic(k):
-            margin = ring.tile([P, 2, P, 2], F32, name="margin")
-            nc.vector.tensor_tensor(margin[:], scores[k][:].rearrange(paired, u=2, e=2), signed[k][:], MULT)
-            sig[k] = ring.tile([P, N], F32, name="sig")
+            c, j = divmod(k, PAIR)
+            margin = ring.tile([P, 2, P, 2], F32, name="margin", bufs=4)
+            nc.vector.tensor_tensor(margin[:], scores[k][:].rearrange(paired, u=2, e=2), signed[c][:, :, j, :, :], MULT)
+            sig[k] = ring.tile([P, N], F32, name="sig", bufs=4)
             nc.scalar.activation(sig[k][:], margin[:].rearrange("p u q e -> p (u q e)"), SIGMOID, scale=-1.0)
 
         def weigh(k):
-            h = ring.tile([P, N], BF16, name="h", align_bytes=64)
+            c, j = divmod(k, PAIR)
+            h = ring.tile([P, N], BF16, name="h", align_bytes=64, bufs=4)
             nc.vector.scalar_tensor_tensor(
-                h[:], sig[k][:], neg_wt[:, k : k + 1], signed[k][:].rearrange("p u q e -> p (u q e)"), MULT, MULT
+                h[:].rearrange("p (u m) -> p u m", u=2),
+                sig[k][:].rearrange("p (u m) -> p u m", u=2),
+                neg_wt[:, k : k + 1],
+                signed[c][:, :, j, :, :].rearrange("p u q e -> p u (q e)"),
+                MULT, MULT,
             )
-            turned = psum.tile([P, PACK, P], F32, name="h_psum", tag="turn", bufs=3)
+            h_psum = psum.tile([P, 2, P], F32, name="h_psum", tag="turn", bufs=2)
             h_words = h[:].bitcast(F32)
             for u in range(2):
-                nc.tensor.transpose(turned[:, u, :], h_words[:, u * P : (u + 1) * P], ident[:])
-            h_turned[k] = ring.tile([P, P * PACK], BF16, name="h_turned", align_bytes=64)
+                nc.tensor.transpose(h_psum[:, u, :], h_words[:, u * P : (u + 1) * P], ident[:])
+            h_turned[k] = ring.tile([P, P * PACK], BF16, name="h_turned", align_bytes=64, bufs=4)
             nc.scalar.copy(
-                h_turned[k][:].bitcast(F32).rearrange("q (r u) -> q r u", u=2),
-                turned[:, 0:2, :].rearrange("q u r -> q r u"),
+                h_turned[k][:].bitcast(F32).rearrange("q (r u) -> q r u", u=2), h_psum[:].rearrange("q u r -> q r u")
             )
 
         def gradient(k):
             h_codes = ring.tile([P, P], U32, name="h_codes", align_bytes=64)
             h_scales = ring.tile([P, P], U8, name="h_scales", align_bytes=64)
             nc.vector.quantize_mx(h_codes[:].bitcast(E5M2), h_scales[:], h_turned[k][:])
-            grad = psum.tile([P, D], F32, name="grad", tag="grad", bufs=2)
+            grads[k] = psum.tile([P, D], F32, name="grad", tag="grad", bufs=2)
             nc.tensor.matmul_mx(
-                grad[:], h_codes[:].bitcast(E5M2), h_scales[:], w2_codes[:].bitcast(E4M3), w2_scales[:],
+                grads[k][:], h_codes[:].bitcast(E5M2), h_scales[:], w2_codes[:].bitcast(E4M3), w2_scales[:],
                 start=True, stop=True,
             )
-            result = ring.tile([P, D], F32, name="result")
-            nc.scalar.copy(result[:], grad[:])
-            nc.sync.dma_start(out[0, k * P : (k + 1) * P, :], result[:])
+
+        def store(k, copy, pieces):
+            result = ring.tile([P, D], F32, name="result", bufs=4)
+            for piece in range(pieces):
+                cols = slice(piece * D // pieces, (piece + 1) * D // pieces)
+                copy(result[:, cols], grads[k][:, cols])
+                nc.sync.dma_start(out[0, k * P : (k + 1) * P, cols], result[:, cols])
 
         score(0)
-        for step in range(TILES + 2):
-            if step + 1 < TILES:
-                score(step + 1)
-            if step < TILES:
-                logistic(step)
-            if step == 0:
-                nc.vector.quantize_mx(
-                    w2_codes[:].bitcast(E4M3), w2_scales[:], w_by_slot[:].rearrange("q p u e s -> q (p u e s)")
-                )
-            if 0 <= step - 1 < TILES:
-                weigh(step - 1)
-            if 0 <= step - 2 < TILES:
-                gradient(step - 2)
+        sign(0)
+        score(1)
+        turn_w(1)
+        logistic(0)
+        logistic(1)
+        sign(1)
+        nc.vector.quantize_mx(
+            w2_codes[:].bitcast(E4M3), w2_scales[:], w_by_slot[:].rearrange("q p u e s -> q (p u e s)")
+        )
+        for k in range(TILES - 2):
+            logistic(k + 2)
+            weigh(k)
+            if k > 0:
+                gradient(k - 1)
+                store(k - 1, nc.scalar.copy, 1)
+            if k % PAIR == PAIR - 1 and k // PAIR + 2 < TILES // PAIR:
+                score(k // PAIR + 2)
+                sign(k // PAIR + 2)
+        weigh(TILES - 2)
+        gradient(TILES - 3)
+        weigh(TILES - 1)
+        store(TILES - 3, nc.scalar.copy, 1)
+        gradient(TILES - 2)
+        gradient(TILES - 1)
+        store(TILES - 2, nc.scalar.copy, 1)
+        store(TILES - 1, nc.vector.tensor_copy, 2)

@@ -34,7 +34,7 @@ def tile_attend_gsig_x_ts_kernel(tc, xT, wT, y, wt, ts, offs, out):
         w_rows = wT.rearrange("(p t) c -> p t c", t=PACK)
         planes = [keep.tile([P, T], F32, name="plane%d" % t) for t in range(PACK)]
         ts_runs = keep.tile([P, T // P], F32, name="ts_runs")
-        nc.scalar.dma_start(ts_runs[:], ts[0].rearrange("(n m) -> n m", n=P))
+        nc.sync.dma_start(ts_runs[:], ts[0].rearrange("(n m) -> n m", n=P))
         nc.sync.dma_start(planes[0][:], w_rows[:, 0, :])
         nc.sync.dma_start(offsets[:], offs)
         for t in range(1, PACK):

@@ -14,6 +14,8 @@ U8 = mybir.dt.uint8
 E4M3 = mybir.dt.float8_e4m3fn_x4
 E5M2 = mybir.dt.float8_e5m2_x4
 MULT = mybir.AluOpType.mult
+MAX = mybir.AluOpType.max
+SUB = mybir.AluOpType.subtract
 COPY = mybir.ActivationFunctionType.Copy
 SIGMOID = mybir.ActivationFunctionType.Sigmoid
 
@@ -21,6 +23,8 @@ P = 128
 PACK = 4
 TILES = R // P
 PAIR = 2
+CH = PAIR * P
+CHUNKS = R // CH
 
 
 def tile_attend_gsig_x_ts_kernel(tc, xT, wT, y, wt, ts, offs, out):
@@ -32,138 +36,151 @@ def tile_attend_gsig_x_ts_kernel(tc, xT, wT, y, wt, ts, offs, out):
 
         offsets = keep.tile([P, N // 16], U16, name="offsets")
         w_rows = wT.rearrange("(p t) c -> p t c", t=PACK)
-        planes = [keep.tile([P, T], F32, name="plane%d" % t) for t in range(PACK)]
-        ts_runs = keep.tile([P, T // P], F32, name="ts_runs")
-        nc.sync.dma_start(ts_runs[:], ts[0].rearrange("(n m) -> n m", n=P))
-        nc.sync.dma_start(planes[0][:], w_rows[:, 0, :])
+        planes = [keep.tile([P, T], F32, name="plane%d" % t, tag="stage%d" % t) for t in range(PACK)]
+        ts_window = keep.tile([P, T], F32, name="ts_window")
+        wt_runs = keep.tile([P, TILES], F32, name="wt_runs")
+        nc.vector.memset(ts_window[:, 0 : T // 2], 0.0)
+        nc.gpsimd.memset(ts_window[:, T // 2 : T], 0.0)
         nc.sync.dma_start(offsets[:], offs)
+        nc.sync.dma_start(wt_runs[:], wt[0].rearrange("(n m) o -> n (m o)", n=P))
+        nc.sync.dma_start(planes[0][:, 0 : T // 2], w_rows[:, 0, 0 : T // 2])
+        nc.sync.dma_start(ts_window[0:1, 0 : T // 2], ts[0:1, 0 : T // 2])
+        nc.sync.dma_start(ts_window[0:1, T // 2 : T], ts[0:1, T // 2 : T])
+        nc.sync.dma_start(planes[0][:, T // 2 : T], w_rows[:, 0, T // 2 : T])
         for t in range(1, PACK):
             nc.sync.dma_start(planes[t][:], w_rows[:, t, :])
 
         x_rows = xT[0].rearrange("(p t) r -> p t r", t=PACK)
         y_rows = y[0].rearrange("(k p) i -> p k i", p=P)
-        x_raw, y_raw = [], []
-        for c in range(TILES // PAIR):
-            x_raw.append(keep.tile([P, PACK, PAIR * P], F32, name="x_raw%d" % c))
-            y_raw.append(keep.tile([P, PAIR, N], F32, name="y_raw%d" % c))
-            nc.sync.dma_start(x_raw[c][:], x_rows[:, :, c * PAIR * P : (c + 1) * PAIR * P])
-            nc.sync.dma_start(y_raw[c][:], y_rows[:, c * PAIR : (c + 1) * PAIR, :])
+        x_raw, y_raw = {}, {}
+
+        def load_x(c, stage):
+            x_raw[c] = stage.rearrange("p (t r) -> p t r", t=PACK)
+            nc.sync.dma_start(x_raw[c], x_rows[:, :, c * CH : (c + 1) * CH])
+
+        def load_y(k, count, stage):
+            view = stage.rearrange("p (j i) -> p j i", j=count)
+            nc.sync.dma_start(view, y_rows[:, k : k + count, :])
+            for j in range(count):
+                y_raw[k + j] = view[:, j, :]
+
+        def stage_tile(slot, width):
+            return keep.tile([P, width], F32, name="staged", tag="stage%d" % slot)
 
         ident = keep.tile([P, P], F32, name="ident")
         make_identity(nc, ident[:])
         warm = keep.tile([P, 1], F32, name="warm")
         nc.scalar.activation(warm[:], ident[:, 0:1], SIGMOID)
 
-        ts_window = keep.tile([P, T], F32, name="ts_window")
-        window_runs = ts_window[:].rearrange("p (n m) -> p n m", n=P)
-        for b in range(T // P // PACK):
-            spread = psum.tile([P, PACK, P], F32, name="spread", tag="scores", bufs=4)
+        neg_wt = keep.tile([P, R], F32, name="neg_wt")
+        wt_view = neg_wt[:].rearrange("p (n m) -> p n m", n=P)
+        for b in range(TILES // PACK):
+            spread = psum.tile([P, PACK, P], F32, name="spread", tag="labels", bufs=3)
             for m in range(PACK):
                 column = b * PACK + m
-                nc.tensor.transpose(spread[:, m, :], ts_runs[:, column : column + 1].to_broadcast([P, P]), ident[:])
-            nc.scalar.copy(window_runs[:, :, b * PACK : (b + 1) * PACK], spread[:].rearrange("p m n -> p n m"))
-
-        wt_rows = keep.tile([P, P], F32, name="wt_rows")
-        nc.gpsimd.memset(wt_rows[:], 0.0)
-        nc.scalar.dma_start(wt_rows[0:TILES, :], wt[0].rearrange("(k p) o -> k (p o)", p=P))
-        wt_turned = psum.tile([P, PACK, P], F32, name="wt_turned", tag="turn", bufs=2)
-        nc.tensor.transpose(wt_turned[:, 0, :], wt_rows[:], ident[:])
-        neg_wt = keep.tile([P, TILES], F32, name="neg_wt")
-        nc.scalar.activation(neg_wt[:], wt_turned[:, 0, 0:TILES], COPY, scale=-1.0)
+                nc.tensor.transpose(spread[:, m, :], wt_runs[:, column : column + 1].to_broadcast([P, P]), ident[:])
+            nc.scalar.activation(
+                wt_view[:, :, b * PACK : (b + 1) * PACK], spread[:].rearrange("p m n -> p n m"), COPY, scale=-1.0
+            )
 
         ts_all = keep.tile([P, N], F32, name="ts_all")
-        ts_pair = keep.tile([P, 2, PAIR, P, 2], F32, name="ts_pair")
-        paired = "p (q u e) -> p u q e"
+        nc.vector.tensor_copy(ts_all[:], ts_window[:].indirect(offsets[:]))
+        ts_turned = psum.tile([P, PACK, P], F32, name="ts_turned", tag="labels", bufs=3)
+        for s in range(PACK):
+            nc.tensor.transpose(ts_turned[:, s, :], ts_all[:, s::PACK], ident[:])
+        ts_col = keep.tile([P, PACK], F32, name="ts_col")
+        nc.scalar.copy(ts_col[:], ts_turned[:, :, 0])
 
-        w_by_d = keep.tile([P, N, PACK], BF16, name="w_by_d", align_bytes=64)
+        factor = [keep.tile([P, PACK, 2 * CH], F32, name="factor%d" % h) for h in range(CHUNKS // 2)]
+
+        w_by_d = keep.tile([P, PACK, P, PACK], BF16, name="w_by_d", align_bytes=64)
         w_by_slot = keep.tile([P, P, 2, 2, PACK], BF16, name="w_by_slot", align_bytes=64)
-        w_words = w_by_d[:].rearrange("p i t -> p (i t)").bitcast(F32).rearrange("p (q s u) -> p q s u", s=PACK, u=2)
+        w_words = w_by_d[:].rearrange("p s q t -> p (s q t)").bitcast(F32).rearrange("p (s q u) -> p s q u", s=PACK, u=2)
 
-        def turn_w(u):
-            w_turned = psum.tile([P, PACK, P], F32, name="w_turned", tag="grad", bufs=2)
+        def make_factor(h):
+            rows = neg_wt[:, 2 * h * CH : 2 * (h + 1) * CH]
             for s in range(PACK):
-                nc.tensor.transpose(w_turned[:, s, :], w_words[:, :, s, u], ident[:])
+                if h == 0:
+                    nc.scalar.activation(factor[h][:, s, :], rows, COPY, scale=ts_col[:, s : s + 1])
+                else:
+                    nc.vector.tensor_scalar(factor[h][:, s, :], rows, ts_col[:, s : s + 1], None, MULT)
+
+        def turn_w(u, bank):
+            w_turned = psum.tile([P, PACK, P], F32, name="w_turned", tag=bank)
+            for s in range(PACK):
+                nc.tensor.transpose(w_turned[:, s, :], w_words[:, s, :, u], ident[:])
             halves = w_turned[:].rearrange("q s p -> q (s p)").bitcast(BF16)
             nc.scalar.copy(w_by_slot[:, :, u, :, :], halves.rearrange("q (s p e) -> q p e s", s=PACK, e=2))
 
         for t in range(PACK):
-            nc.vector.tensor_copy(w_by_d[:, :, t], planes[t][:].indirect(offsets[:]))
+            nc.vector.tensor_copy(w_by_d[:, :, :, t].rearrange("p s q -> p q s"), planes[t][:].indirect(offsets[:]))
+            if t == 0:
+                make_factor(0)
             if t == 1:
-                nc.vector.tensor_copy(ts_all[:], ts_window[:].indirect(offsets[:]))
-                for j in range(PAIR):
-                    nc.scalar.copy(ts_pair[:, :, j, :, :], ts_all[:].rearrange(paired, u=2, e=2))
-                turn_w(0)
+                turn_w(0, "score2")
+                make_factor(1)
         w1_codes = keep.tile([P, N], U32, name="w1_codes", align_bytes=64)
         w1_scales = keep.tile([P, N], U8, name="w1_scales", align_bytes=64)
-        nc.vector.quantize_mx(w1_codes[:].bitcast(E4M3), w1_scales[:], w_by_d[:].rearrange("p i t -> p (i t)"))
+        nc.vector.quantize_mx(w1_codes[:].bitcast(E4M3), w1_scales[:], w_by_d[:].rearrange("p s q t -> p (s q t)"))
         w2_codes = keep.tile([P, D], U32, name="w2_codes", align_bytes=64)
         w2_scales = keep.tile([P, D], U8, name="w2_scales", align_bytes=64)
 
-        scores, signed, sig, h_turned, grads = {}, {}, {}, {}, {}
+        x_mx, probs, labels, h_bf, grads = {}, {}, {}, {}, {}
+
+        def prepare_x(c):
+            x_bf = ring.tile([P, CH, PACK], BF16, name="x_bf", align_bytes=64, bufs=1)
+            copy = nc.vector.tensor_copy if c == 1 else nc.scalar.copy
+            copy(
+                x_bf[:].rearrange("p (c i) t -> p c t i", i=4),
+                x_raw[c].rearrange("p t (c i) -> p c t i", i=4),
+            )
+            x_codes = ring.tile([P, CH], U32, name="x_codes", align_bytes=64, bufs=2)
+            x_scales = ring.tile([P, CH], U8, name="x_scales", align_bytes=64)
+            nc.vector.quantize_mx(x_codes[:].bitcast(E4M3), x_scales[:], x_bf[:].rearrange("p r t -> p (r t)"))
+            x_mx[c] = (x_codes, x_scales)
 
         def score(c):
-            x_bf = ring.tile([P, PAIR * P, PACK], BF16, name="x_bf", align_bytes=64)
-            nc.scalar.copy(
-                x_bf[:].rearrange("p (c i) t -> p c t i", i=4),
-                x_raw[c][:].rearrange("p t (c i) -> p c t i", i=4),
-            )
-            x_codes = ring.tile([P, PAIR * P], U32, name="x_codes", align_bytes=64)
-            x_scales = ring.tile([P, PAIR * P], U8, name="x_scales", align_bytes=64)
-            nc.vector.quantize_mx(x_codes[:].bitcast(E4M3), x_scales[:], x_bf[:].rearrange("p r t -> p (r t)"))
-            for j in range(PAIR):
-                k = c * PAIR + j
-                rows = slice(j * P, (j + 1) * P)
-                scores[k] = psum.tile([P, N], F32, name="scores", tag="scores", bufs=4)
-                nc.tensor.matmul_mx(
-                    scores[k][:], x_codes[:, rows].bitcast(E4M3), x_scales[:, rows],
-                    w1_codes[:].bitcast(E4M3), w1_scales[:], start=True, stop=True,
-                )
-
-        def sign(c):
-            signed[c] = ring.tile([P, 2, PAIR, P, 2], F32, name="signed", bufs=4)
-            if c == 0:
-                for j in range(PAIR):
-                    nc.vector.tensor_tensor(
-                        signed[c][:, :, j, :, :], y_raw[c][:, j, :].rearrange(paired, u=2, e=2), ts_pair[:, :, j, :, :], MULT
+            x_codes, x_scales = x_mx[c]
+            probs[c] = ring.tile([P, PACK, CH], F32, name="probs", bufs=2)
+            for b in range(2):
+                scores = psum.tile([P, 2, CH], F32, name="scores", tag="score%d" % ((2 * c + b) % 3))
+                for e in range(2):
+                    cols = slice((2 * b + e) * P, (2 * b + e + 1) * P)
+                    nc.tensor.matmul_mx(
+                        scores[:, e, :], w1_codes[:, cols].bitcast(E4M3), w1_scales[:, cols],
+                        x_codes[:].bitcast(E4M3), x_scales[:], start=True, stop=True,
                     )
-            else:
-                nc.vector.tensor_tensor(
-                    signed[c][:].rearrange("p u j q e -> p u (j q) e"),
-                    y_raw[c][:].rearrange("p j (q u e) -> p u (j q) e", u=2, e=2),
-                    ts_pair[:].rearrange("p u j q e -> p u (j q) e"),
-                    MULT,
-                )
+                for e in range(2):
+                    s = 2 * b + e
+                    nc.scalar.activation(probs[c][:, s, :], scores[:, e, :], SIGMOID, scale=ts_col[:, s : s + 1])
 
-        def logistic(k):
-            c, j = divmod(k, PAIR)
-            margin = ring.tile([P, 2, P, 2], F32, name="margin", bufs=4)
-            nc.vector.tensor_tensor(margin[:], scores[k][:].rearrange(paired, u=2, e=2), signed[c][:, :, j, :, :], MULT)
-            sig[k] = ring.tile([P, N], F32, name="sig", bufs=4)
-            nc.scalar.activation(sig[k][:], margin[:].rearrange("p u q e -> p (u q e)"), SIGMOID, scale=-1.0)
+        def turn_y(k):
+            labels[k] = psum.tile([P, PACK, P], F32, name="labels", tag="labels", bufs=3)
+            for s in range(PACK):
+                nc.tensor.transpose(labels[k][:, s, :], y_raw[k][:, s::PACK], ident[:])
 
         def weigh(k):
             c, j = divmod(k, PAIR)
-            h = ring.tile([P, N], BF16, name="h", align_bytes=64, bufs=4)
-            nc.vector.scalar_tensor_tensor(
-                h[:].rearrange("p (u m) -> p u m", u=2),
-                sig[k][:].rearrange("p (u m) -> p u m", u=2),
-                neg_wt[:, k : k + 1],
-                signed[c][:, :, j, :, :].rearrange("p u q e -> p u (q e)"),
-                MULT, MULT,
-            )
-            h_psum = psum.tile([P, 2, P], F32, name="h_psum", tag="turn", bufs=2)
-            h_words = h[:].bitcast(F32)
-            for u in range(2):
-                nc.tensor.transpose(h_psum[:, u, :], h_words[:, u * P : (u + 1) * P], ident[:])
-            h_turned[k] = ring.tile([P, P * PACK], BF16, name="h_turned", align_bytes=64, bufs=4)
-            nc.scalar.copy(
-                h_turned[k][:].bitcast(F32).rearrange("q (r u) -> q r u", u=2), h_psum[:].rearrange("q u r -> q r u")
+            rows = slice(j * P, (j + 1) * P)
+            diff = ring.tile([P, PACK, P], F32, name="diff", bufs=3)
+            nc.vector.scalar_tensor_tensor(diff[:], labels[k][:], 0.0, probs[c][:, :, rows], MAX, SUB)
+            return diff
+
+        def scale(k, diff):
+            c, j = divmod(k, PAIR)
+            rows = slice(k % 4 * P, (k % 4 + 1) * P)
+            h_bf[k] = ring.tile([P, P, PACK], BF16, name="h_bf", align_bytes=64, bufs=3)
+            nc.vector.tensor_tensor(
+                h_bf[k][:].rearrange("q (c i) s -> q c s i", i=4),
+                diff[:].rearrange("q s (c i) -> q c s i", i=4),
+                factor[k // 4][:, :, rows].rearrange("q s (c i) -> q c s i", i=4),
+                MULT,
             )
 
         def gradient(k):
             h_codes = ring.tile([P, P], U32, name="h_codes", align_bytes=64)
             h_scales = ring.tile([P, P], U8, name="h_scales", align_bytes=64)
-            nc.vector.quantize_mx(h_codes[:].bitcast(E5M2), h_scales[:], h_turned[k][:])
+            nc.vector.quantize_mx(h_codes[:].bitcast(E5M2), h_scales[:], h_bf[k][:].rearrange("q r s -> q (r s)"))
             grads[k] = psum.tile([P, D], F32, name="grad", tag="grad", bufs=2)
             nc.tensor.matmul_mx(
                 grads[k][:], h_codes[:].bitcast(E5M2), h_scales[:], w2_codes[:].bitcast(E4M3), w2_scales[:],
@@ -177,30 +194,41 @@ def tile_attend_gsig_x_ts_kernel(tc, xT, wT, y, wt, ts, offs, out):
                 copy(result[:, cols], grads[k][:, cols])
                 nc.sync.dma_start(out[0, k * P : (k + 1) * P, cols], result[:, cols])
 
+        load_y(0, 1, stage_tile(0, N)[:])
+        load_x(0, stage_tile(1, PACK * CH)[:])
+        both = stage_tile(2, N + PACK * CH)
+        load_y(1, 1, both[:, 0:N])
+        load_x(1, both[:, N : N + PACK * CH])
+        rest = stage_tile(3, 5 * PAIR * N)
+        load_y(2, PAIR, rest[:, 0:1024])
+        load_x(2, rest[:, 1024:2048])
+        load_y(4, PAIR, rest[:, 2048:3072])
+        load_x(3, rest[:, 3072:4096])
+        load_y(6, PAIR, rest[:, 4096:5120])
+        turn_y(0)
+        turn_y(1)
+        prepare_x(0)
         score(0)
-        sign(0)
-        score(1)
-        turn_w(1)
-        logistic(0)
-        logistic(1)
-        sign(1)
+        prepare_x(1)
+        turn_w(1, "score0")
         nc.vector.quantize_mx(
             w2_codes[:].bitcast(E4M3), w2_scales[:], w_by_slot[:].rearrange("q p u e s -> q (p u e s)")
         )
-        for k in range(TILES - 2):
-            logistic(k + 2)
-            weigh(k)
-            if k > 0:
-                gradient(k - 1)
-                store(k - 1, nc.scalar.copy, 1)
-            if k % PAIR == PAIR - 1 and k // PAIR + 2 < TILES // PAIR:
-                score(k // PAIR + 2)
-                sign(k // PAIR + 2)
-        weigh(TILES - 2)
-        gradient(TILES - 3)
-        weigh(TILES - 1)
-        store(TILES - 3, nc.scalar.copy, 1)
-        gradient(TILES - 2)
-        gradient(TILES - 1)
-        store(TILES - 2, nc.scalar.copy, 1)
-        store(TILES - 1, nc.vector.tensor_copy, 2)
+        for c in range(CHUNKS):
+            a, b = PAIR * c, PAIR * c + 1
+            if c + 1 < CHUNKS:
+                score(c + 1)
+            diff_a = weigh(a)
+            diff_b = weigh(b)
+            if c + 1 < CHUNKS:
+                turn_y(a + 2)
+                turn_y(b + 2)
+            if c + 2 < CHUNKS:
+                prepare_x(c + 2)
+            scale(a, diff_a)
+            scale(b, diff_b)
+            gradient(a)
+            gradient(b)
+            last = c == CHUNKS - 1
+            store(a, nc.scalar.copy, 1)
+            store(b, nc.vector.tensor_copy if last else nc.scalar.copy, 2 if last else 1)

@@ -22,9 +22,8 @@ SIGMOID = mybir.ActivationFunctionType.Sigmoid
 P = 128
 PACK = 4
 TILES = R // P
-PAIR = 2
-CH = PAIR * P
-CHUNKS = R // CH
+HALF = R // 2
+CHUNKS = [(0,), (1, 2), (3, 4), (5, 6), (7,)]
 
 
 def tile_attend_gsig_x_ts_kernel(tc, xT, wT, y, wt, ts, offs, out):
@@ -36,27 +35,27 @@ def tile_attend_gsig_x_ts_kernel(tc, xT, wT, y, wt, ts, offs, out):
 
         offsets = keep.tile([P, N // 16], U16, name="offsets")
         w_rows = wT.rearrange("(p t) c -> p t c", t=PACK)
-        planes = [keep.tile([P, T], F32, name="plane%d" % t, tag="stage%d" % t) for t in range(PACK)]
+        planes = [keep.tile([P, T], F32, name="plane%d" % t, tag="stage%d" % t, align_bytes=64) for t in range(PACK)]
         ts_window = keep.tile([P, T], F32, name="ts_window")
         wt_runs = keep.tile([P, TILES], F32, name="wt_runs")
         nc.vector.memset(ts_window[:, 0 : T // 2], 0.0)
         nc.gpsimd.memset(ts_window[:, T // 2 : T], 0.0)
-        nc.sync.dma_start(offsets[:], offs)
         nc.sync.dma_start(wt_runs[:], wt[0].rearrange("(n m) o -> n (m o)", n=P))
         nc.sync.dma_start(planes[0][:, 0 : T // 2], w_rows[:, 0, 0 : T // 2])
+        nc.sync.dma_start(offsets[:], offs)
         nc.sync.dma_start(ts_window[0:1, 0 : T // 2], ts[0:1, 0 : T // 2])
         nc.sync.dma_start(ts_window[0:1, T // 2 : T], ts[0:1, T // 2 : T])
         nc.sync.dma_start(planes[0][:, T // 2 : T], w_rows[:, 0, T // 2 : T])
-        for t in range(1, PACK):
-            nc.sync.dma_start(planes[t][:], w_rows[:, t, :])
-
         x_rows = xT[0].rearrange("(p t) r -> p t r", t=PACK)
         y_rows = y[0].rearrange("(k p) i -> p k i", p=P)
         x_raw, y_raw = {}, {}
 
-        def load_x(c, stage):
-            x_raw[c] = stage.rearrange("p (t r) -> p t r", t=PACK)
-            nc.sync.dma_start(x_raw[c], x_rows[:, :, c * CH : (c + 1) * CH])
+        def load_x(k, count, stage):
+            view = stage.rearrange("p (t r) -> p t r", t=PACK)
+            nc.sync.dma_start(view, x_rows[:, :, k * P : (k + count) * P])
+            for c, tiles in enumerate(CHUNKS):
+                if k <= tiles[0] < k + count:
+                    x_raw[c] = view[:, :, (tiles[0] - k) * P : (tiles[-1] + 1 - k) * P]
 
         def load_y(k, count, stage):
             view = stage.rearrange("p (j i) -> p j i", j=count)
@@ -64,8 +63,10 @@ def tile_attend_gsig_x_ts_kernel(tc, xT, wT, y, wt, ts, offs, out):
             for j in range(count):
                 y_raw[k + j] = view[:, j, :]
 
-        def stage_tile(slot, width):
-            return keep.tile([P, width], F32, name="staged", tag="stage%d" % slot)
+        first_y = keep.tile([P, N], F32, name="first_y")
+        for t in range(1, PACK):
+            nc.sync.dma_start(planes[t][:], w_rows[:, t, :])
+        load_y(0, 1, first_y[:])
 
         ident = keep.tile([P, P], F32, name="ident")
         make_identity(nc, ident[:])
@@ -75,7 +76,7 @@ def tile_attend_gsig_x_ts_kernel(tc, xT, wT, y, wt, ts, offs, out):
         neg_wt = keep.tile([P, R], F32, name="neg_wt")
         wt_view = neg_wt[:].rearrange("p (n m) -> p n m", n=P)
         for b in range(TILES // PACK):
-            spread = psum.tile([P, PACK, P], F32, name="spread", tag="labels", bufs=3)
+            spread = psum.tile([P, PACK, P], F32, name="spread", tag="label%d" % b)
             for m in range(PACK):
                 column = b * PACK + m
                 nc.tensor.transpose(spread[:, m, :], wt_runs[:, column : column + 1].to_broadcast([P, P]), ident[:])
@@ -85,89 +86,86 @@ def tile_attend_gsig_x_ts_kernel(tc, xT, wT, y, wt, ts, offs, out):
 
         ts_all = keep.tile([P, N], F32, name="ts_all")
         nc.vector.tensor_copy(ts_all[:], ts_window[:].indirect(offsets[:]))
-        ts_turned = psum.tile([P, PACK, P], F32, name="ts_turned", tag="labels", bufs=3)
+        ts_turned = psum.tile([P, PACK, P], F32, name="ts_turned", tag="label2")
         for s in range(PACK):
             nc.tensor.transpose(ts_turned[:, s, :], ts_all[:, s::PACK], ident[:])
         ts_col = keep.tile([P, PACK], F32, name="ts_col")
         nc.scalar.copy(ts_col[:], ts_turned[:, :, 0])
 
-        factor = [keep.tile([P, PACK, 2 * CH], F32, name="factor%d" % h) for h in range(CHUNKS // 2)]
+        factor = [keep.tile([P, PACK, HALF], F32, name="factor%d" % h) for h in range(2)]
 
         w_by_d = keep.tile([P, PACK, P, PACK], BF16, name="w_by_d", align_bytes=64)
-        w_by_slot = keep.tile([P, P, 2, 2, PACK], BF16, name="w_by_slot", align_bytes=64)
         w_words = w_by_d[:].rearrange("p s q t -> p (s q t)").bitcast(F32).rearrange("p (s q u) -> p s q u", s=PACK, u=2)
 
         def make_factor(h):
-            rows = neg_wt[:, 2 * h * CH : 2 * (h + 1) * CH]
+            rows = neg_wt[:, h * HALF : (h + 1) * HALF]
             for s in range(PACK):
-                if h == 0:
-                    nc.scalar.activation(factor[h][:, s, :], rows, COPY, scale=ts_col[:, s : s + 1])
-                else:
+                if h == 1:
                     nc.vector.tensor_scalar(factor[h][:, s, :], rows, ts_col[:, s : s + 1], None, MULT)
+                else:
+                    nc.scalar.activation(factor[h][:, s, :], rows, COPY, scale=ts_col[:, s : s + 1])
 
-        def turn_w(u, bank):
+        def turn_w(u, bank, pool, stage):
             w_turned = psum.tile([P, PACK, P], F32, name="w_turned", tag=bank)
             for s in range(PACK):
                 nc.tensor.transpose(w_turned[:, s, :], w_words[:, s, :, u], ident[:])
             halves = w_turned[:].rearrange("q s p -> q (s p)").bitcast(BF16)
-            nc.scalar.copy(w_by_slot[:, :, u, :, :], halves.rearrange("q (s p e) -> q p e s", s=PACK, e=2))
+            w_by_slot = pool.tile([P, P, 2, PACK], BF16, name="w_by_slot", tag=stage, align_bytes=64, bufs=1)
+            nc.scalar.copy(w_by_slot[:], halves.rearrange("q (s p e) -> q p e s", s=PACK, e=2))
+            cols = slice(u * D // 2, (u + 1) * D // 2)
+            nc.vector.quantize_mx(
+                w2_codes[:, cols].bitcast(E4M3), w2_scales[:, cols], w_by_slot[:].rearrange("q p e s -> q (p e s)")
+            )
 
-        for t in range(PACK):
-            nc.vector.tensor_copy(w_by_d[:, :, :, t].rearrange("p s q -> p q s"), planes[t][:].indirect(offsets[:]))
-            if t == 0:
-                make_factor(0)
-            if t == 1:
-                turn_w(0, "score2")
-                make_factor(1)
         w1_codes = keep.tile([P, N], U32, name="w1_codes", align_bytes=64)
         w1_scales = keep.tile([P, N], U8, name="w1_scales", align_bytes=64)
-        nc.vector.quantize_mx(w1_codes[:].bitcast(E4M3), w1_scales[:], w_by_d[:].rearrange("p s q t -> p (s q t)"))
         w2_codes = keep.tile([P, D], U32, name="w2_codes", align_bytes=64)
         w2_scales = keep.tile([P, D], U8, name="w2_scales", align_bytes=64)
 
         x_mx, probs, labels, h_bf, grads = {}, {}, {}, {}, {}
 
-        def prepare_x(c):
-            x_bf = ring.tile([P, CH, PACK], BF16, name="x_bf", align_bytes=64, bufs=1)
-            copy = nc.vector.tensor_copy if c == 1 else nc.scalar.copy
+        def prepare_x(c, copy):
+            width = len(CHUNKS[c]) * P
+            x_bf = ring.tile([P, width, PACK], BF16, name="x_bf", tag="x%d" % (max(c, 1) % 2), align_bytes=64, bufs=1)
             copy(
                 x_bf[:].rearrange("p (c i) t -> p c t i", i=4),
                 x_raw[c].rearrange("p t (c i) -> p c t i", i=4),
             )
-            x_codes = ring.tile([P, CH], U32, name="x_codes", align_bytes=64, bufs=2)
-            x_scales = ring.tile([P, CH], U8, name="x_scales", align_bytes=64)
+            x_codes = ring.tile([P, width], U32, name="x_codes", tag="x%d" % ((c + 1) % 2 if c else 2), align_bytes=64, bufs=1)
+            x_scales = ring.tile([P, width], U8, name="x_scales", align_bytes=64)
             nc.vector.quantize_mx(x_codes[:].bitcast(E4M3), x_scales[:], x_bf[:].rearrange("p r t -> p (r t)"))
             x_mx[c] = (x_codes, x_scales)
 
-        def score(c):
+        def score(c, banks):
             x_codes, x_scales = x_mx[c]
-            probs[c] = ring.tile([P, PACK, CH], F32, name="probs", bufs=2)
-            for b in range(2):
-                scores = psum.tile([P, 2, CH], F32, name="scores", tag="score%d" % ((2 * c + b) % 3))
-                for e in range(2):
-                    cols = slice((2 * b + e) * P, (2 * b + e + 1) * P)
+            width = len(CHUNKS[c]) * P
+            share = PACK // len(banks)
+            chunk_probs = ring.tile([P, PACK, width], F32, name="probs", bufs=2)
+            for b, bank in enumerate(banks):
+                scores = psum.tile([P, share, width], F32, name="scores", tag=bank)
+                for e in range(share):
+                    cols = slice((share * b + e) * P, (share * b + e + 1) * P)
                     nc.tensor.matmul_mx(
                         scores[:, e, :], w1_codes[:, cols].bitcast(E4M3), w1_scales[:, cols],
                         x_codes[:].bitcast(E4M3), x_scales[:], start=True, stop=True,
                     )
-                for e in range(2):
-                    s = 2 * b + e
-                    nc.scalar.activation(probs[c][:, s, :], scores[:, e, :], SIGMOID, scale=ts_col[:, s : s + 1])
+                for e in range(share):
+                    s = share * b + e
+                    nc.scalar.activation(chunk_probs[:, s, :], scores[:, e, :], SIGMOID, scale=ts_col[:, s : s + 1])
+            for j, k in enumerate(CHUNKS[c]):
+                probs[k] = chunk_probs[:, :, j * P : (j + 1) * P]
 
         def turn_y(k):
-            labels[k] = psum.tile([P, PACK, P], F32, name="labels", tag="labels", bufs=3)
+            labels[k] = psum.tile([P, PACK, P], F32, name="labels", tag="label%d" % ((k + 2) % 3))
             for s in range(PACK):
                 nc.tensor.transpose(labels[k][:, s, :], y_raw[k][:, s::PACK], ident[:])
 
         def weigh(k):
-            c, j = divmod(k, PAIR)
-            rows = slice(j * P, (j + 1) * P)
             diff = ring.tile([P, PACK, P], F32, name="diff", bufs=3)
-            nc.vector.scalar_tensor_tensor(diff[:], labels[k][:], 0.0, probs[c][:, :, rows], MAX, SUB)
+            nc.vector.scalar_tensor_tensor(diff[:], labels[k][:], 0.0, probs[k], MAX, SUB)
             return diff
 
         def scale(k, diff):
-            c, j = divmod(k, PAIR)
             rows = slice(k % 4 * P, (k % 4 + 1) * P)
             h_bf[k] = ring.tile([P, P, PACK], BF16, name="h_bf", align_bytes=64, bufs=3)
             nc.vector.tensor_tensor(
@@ -189,46 +187,55 @@ def tile_attend_gsig_x_ts_kernel(tc, xT, wT, y, wt, ts, offs, out):
 
         def store(k, copy, pieces):
             result = ring.tile([P, D], F32, name="result", bufs=4)
+            ordered = grads[k][:].rearrange("r (u p e) -> r p u e", u=2, e=2)
             for piece in range(pieces):
                 cols = slice(piece * D // pieces, (piece + 1) * D // pieces)
-                copy(result[:, cols], grads[k][:, cols])
+                copy(
+                    result[:, cols].rearrange("r (p u e) -> r p u e", u=2, e=2),
+                    ordered[:, piece * P // pieces : (piece + 1) * P // pieces, :, :],
+                )
                 nc.sync.dma_start(out[0, k * P : (k + 1) * P, cols], result[:, cols])
 
-        load_y(0, 1, stage_tile(0, N)[:])
-        load_x(0, stage_tile(1, PACK * CH)[:])
-        both = stage_tile(2, N + PACK * CH)
-        load_y(1, 1, both[:, 0:N])
-        load_x(1, both[:, N : N + PACK * CH])
-        rest = stage_tile(3, 5 * PAIR * N)
-        load_y(2, PAIR, rest[:, 0:1024])
-        load_x(2, rest[:, 1024:2048])
-        load_y(4, PAIR, rest[:, 2048:3072])
-        load_x(3, rest[:, 3072:4096])
-        load_y(6, PAIR, rest[:, 4096:5120])
+        def gather(t):
+            nc.vector.tensor_copy(w_by_d[:, :, :, t].rearrange("p s q -> p q s"), planes[t][:].indirect(offsets[:]))
+
+        gather(0)
+        make_factor(0)
+        gather(1)
+        turn_w(0, "score0", keep, "stage0")
+        first_x = keep.tile([P, N], F32, name="first_x", tag="stage1", align_bytes=64)
+        load_x(0, 1, first_x[:])
+        gather(2)
+        make_factor(1)
+        second = keep.tile([P, 4 * N], F32, name="second", tag="stage2", align_bytes=64)
+        load_x(1, 2, second[:, 0 : 2 * N])
+        load_y(1, 2, second[:, 2 * N : 4 * N])
         turn_y(0)
-        turn_y(1)
-        prepare_x(0)
-        score(0)
-        prepare_x(1)
-        turn_w(1, "score0")
-        nc.vector.quantize_mx(
-            w2_codes[:].bitcast(E4M3), w2_scales[:], w_by_slot[:].rearrange("q p u e s -> q (p u e s)")
-        )
-        for c in range(CHUNKS):
-            a, b = PAIR * c, PAIR * c + 1
-            if c + 1 < CHUNKS:
-                score(c + 1)
-            diff_a = weigh(a)
-            diff_b = weigh(b)
-            if c + 1 < CHUNKS:
-                turn_y(a + 2)
-                turn_y(b + 2)
-            if c + 2 < CHUNKS:
-                prepare_x(c + 2)
-            scale(a, diff_a)
-            scale(b, diff_b)
-            gradient(a)
-            gradient(b)
-            last = c == CHUNKS - 1
-            store(a, nc.scalar.copy, 1)
-            store(b, nc.vector.tensor_copy if last else nc.scalar.copy, 2 if last else 1)
+        gather(3)
+        rest = keep.tile([P, 10 * N], F32, name="rest", tag="stage3", align_bytes=64)
+        load_x(3, 2, rest[:, 0 : 2 * N])
+        load_y(3, 2, rest[:, 2 * N : 4 * N])
+        load_x(5, 3, rest[:, 4 * N : 7 * N])
+        load_y(5, 2, rest[:, 7 * N : 9 * N])
+        load_y(7, 1, rest[:, 9 * N : 10 * N])
+        nc.vector.quantize_mx(w1_codes[:].bitcast(E4M3), w1_scales[:], w_by_d[:].rearrange("p s q t -> p (s q t)"))
+        prepare_x(0, nc.scalar.copy)
+        score(0, ("label0", "label1"))
+        prepare_x(1, nc.vector.tensor_copy)
+        turn_w(1, "score2", ring, "x2")
+        for c, tiles in enumerate(CHUNKS):
+            if c + 1 < len(CHUNKS):
+                score(c + 1, ("score%d" % ((2 * c) % 3), "score%d" % ((2 * c + 1) % 3)))
+            diffs = [weigh(k) for k in tiles]
+            if c + 1 < len(CHUNKS):
+                for k in CHUNKS[c + 1]:
+                    turn_y(k)
+            if c + 2 < len(CHUNKS):
+                prepare_x(c + 2, nc.scalar.copy if c else nc.vector.tensor_copy)
+            for k, diff in zip(tiles, diffs):
+                scale(k, diff)
+            for k in tiles:
+                gradient(k)
+            for k in tiles:
+                last = k == TILES - 1
+                store(k, nc.vector.tensor_copy if last else nc.scalar.copy, 2 if last else 1)

@@ -23,7 +23,10 @@ P = 128
 PACK = 4
 TILES = R // P
 HALF = R // 2
-CHUNKS = [(0,), (1, 2), (3, 4), (5, 6), (7,)]
+CHUNKS = [(0,), (1,), (2, 3), (4, 5), (6,), (7,)]
+LABEL_BANKS = ["label2", "grad1", "label0", "label1", "label2", "label0", "label1", "label2"]
+CAST_TAGS = ["x0", "x0", "x0", "x1", "x0", "x2"]
+CODE_TAGS = ["x2", "x3", "x1", "x0", "x1", "x3"]
 
 
 def tile_attend_gsig_x_ts_kernel(tc, xT, wT, y, wt, ts, offs, out):
@@ -63,26 +66,28 @@ def tile_attend_gsig_x_ts_kernel(tc, xT, wT, y, wt, ts, offs, out):
             for j in range(count):
                 y_raw[k + j] = view[:, j, :]
 
-        first_y = keep.tile([P, N], F32, name="first_y")
+        first_y = keep.tile([P, 2 * N], F32, name="first_y")
         for t in range(1, PACK):
             nc.sync.dma_start(planes[t][:], w_rows[:, t, :])
-        load_y(0, 1, first_y[:])
+        load_y(0, 1, first_y[:, 0:N])
+        load_y(1, 1, first_y[:, N : 2 * N])
 
         ident = keep.tile([P, P], F32, name="ident")
         make_identity(nc, ident[:])
         warm = keep.tile([P, 1], F32, name="warm")
         nc.scalar.activation(warm[:], ident[:, 0:1], SIGMOID)
 
-        neg_wt = keep.tile([P, R], F32, name="neg_wt")
-        wt_view = neg_wt[:].rearrange("p (n m) -> p n m", n=P)
+        neg_wt = [keep.tile([P, HALF], F32, name="neg_wt", tag="wt%d" % h, align_bytes=64) for h in range(2)]
         for b in range(TILES // PACK):
             spread = psum.tile([P, PACK, P], F32, name="spread", tag="label%d" % b)
             for m in range(PACK):
                 column = b * PACK + m
                 nc.tensor.transpose(spread[:, m, :], wt_runs[:, column : column + 1].to_broadcast([P, P]), ident[:])
-            nc.scalar.activation(
-                wt_view[:, :, b * PACK : (b + 1) * PACK], spread[:].rearrange("p m n -> p n m"), COPY, scale=-1.0
-            )
+            for h in range(2):
+                nc.scalar.activation(
+                    neg_wt[h][:].rearrange("p (n m) -> p n m", m=TILES)[:, :, b * PACK : (b + 1) * PACK],
+                    spread[:, :, h * P // 2 : (h + 1) * P // 2].rearrange("p m n -> p n m"), COPY, scale=-1.0,
+                )
 
         ts_all = keep.tile([P, N], F32, name="ts_all")
         nc.vector.tensor_copy(ts_all[:], ts_window[:].indirect(offsets[:]))
@@ -98,12 +103,9 @@ def tile_attend_gsig_x_ts_kernel(tc, xT, wT, y, wt, ts, offs, out):
         w_words = w_by_d[:].rearrange("p s q t -> p (s q t)").bitcast(F32).rearrange("p (s q u) -> p s q u", s=PACK, u=2)
 
         def make_factor(h):
-            rows = neg_wt[:, h * HALF : (h + 1) * HALF]
+            rows = neg_wt[h][:]
             for s in range(PACK):
-                if h == 1:
-                    nc.vector.tensor_scalar(factor[h][:, s, :], rows, ts_col[:, s : s + 1], None, MULT)
-                else:
-                    nc.scalar.activation(factor[h][:, s, :], rows, COPY, scale=ts_col[:, s : s + 1])
+                nc.scalar.activation(factor[h][:, s, :], rows, COPY, scale=ts_col[:, s : s + 1])
 
         def turn_w(u, bank, pool, stage):
             w_turned = psum.tile([P, PACK, P], F32, name="w_turned", tag=bank)
@@ -126,12 +128,12 @@ def tile_attend_gsig_x_ts_kernel(tc, xT, wT, y, wt, ts, offs, out):
 
         def prepare_x(c, copy):
             width = len(CHUNKS[c]) * P
-            x_bf = ring.tile([P, width, PACK], BF16, name="x_bf", tag="x%d" % (max(c, 1) % 2), align_bytes=64, bufs=1)
+            x_bf = ring.tile([P, width, PACK], BF16, name="x_bf", tag=CAST_TAGS[c], align_bytes=64, bufs=1)
             copy(
                 x_bf[:].rearrange("p (c i) t -> p c t i", i=4),
                 x_raw[c].rearrange("p t (c i) -> p c t i", i=4),
             )
-            x_codes = ring.tile([P, width], U32, name="x_codes", tag="x%d" % ((c + 1) % 2 if c else 2), align_bytes=64, bufs=1)
+            x_codes = ring.tile([P, width], U32, name="x_codes", tag=CODE_TAGS[c], align_bytes=64, bufs=1)
             x_scales = ring.tile([P, width], U8, name="x_scales", align_bytes=64)
             nc.vector.quantize_mx(x_codes[:].bitcast(E4M3), x_scales[:], x_bf[:].rearrange("p r t -> p (r t)"))
             x_mx[c] = (x_codes, x_scales)
@@ -156,7 +158,7 @@ def tile_attend_gsig_x_ts_kernel(tc, xT, wT, y, wt, ts, offs, out):
                 probs[k] = chunk_probs[:, :, j * P : (j + 1) * P]
 
         def turn_y(k):
-            labels[k] = psum.tile([P, PACK, P], F32, name="labels", tag="label%d" % ((k + 2) % 3))
+            labels[k] = psum.tile([P, PACK, P], F32, name="labels", tag=LABEL_BANKS[k])
             for s in range(PACK):
                 nc.tensor.transpose(labels[k][:, s, :], y_raw[k][:, s::PACK], ident[:])
 
@@ -179,7 +181,7 @@ def tile_attend_gsig_x_ts_kernel(tc, xT, wT, y, wt, ts, offs, out):
             h_codes = ring.tile([P, P], U32, name="h_codes", align_bytes=64)
             h_scales = ring.tile([P, P], U8, name="h_scales", align_bytes=64)
             nc.vector.quantize_mx(h_codes[:].bitcast(E5M2), h_scales[:], h_bf[k][:].rearrange("q r s -> q (r s)"))
-            grads[k] = psum.tile([P, D], F32, name="grad", tag="grad", bufs=2)
+            grads[k] = psum.tile([P, D], F32, name="grad", tag="grad%d" % (k % 3))
             nc.tensor.matmul_mx(
                 grads[k][:], h_codes[:].bitcast(E5M2), h_scales[:], w2_codes[:].bitcast(E4M3), w2_scales[:],
                 start=True, stop=True,
@@ -202,40 +204,43 @@ def tile_attend_gsig_x_ts_kernel(tc, xT, wT, y, wt, ts, offs, out):
         gather(0)
         make_factor(0)
         gather(1)
-        turn_w(0, "score0", keep, "stage0")
+        turn_w(0, "score0", keep, "wt0")
         first_x = keep.tile([P, N], F32, name="first_x", tag="stage1", align_bytes=64)
         load_x(0, 1, first_x[:])
         gather(2)
         make_factor(1)
-        second = keep.tile([P, 4 * N], F32, name="second", tag="stage2", align_bytes=64)
-        load_x(1, 2, second[:, 0 : 2 * N])
-        load_y(1, 2, second[:, 2 * N : 4 * N])
+        second = keep.tile([P, 3 * N], F32, name="second", tag="stage2", align_bytes=64)
+        load_x(1, 1, second[:, 0:N])
+        load_x(2, 2, second[:, N : 3 * N])
         turn_y(0)
+        turn_y(1)
         gather(3)
         rest = keep.tile([P, 10 * N], F32, name="rest", tag="stage3", align_bytes=64)
-        load_x(3, 2, rest[:, 0 : 2 * N])
-        load_y(3, 2, rest[:, 2 * N : 4 * N])
-        load_x(5, 3, rest[:, 4 * N : 7 * N])
-        load_y(5, 2, rest[:, 7 * N : 9 * N])
-        load_y(7, 1, rest[:, 9 * N : 10 * N])
+        load_y(2, 2, rest[:, 0 : 2 * N])
+        load_x(4, 2, rest[:, 2 * N : 4 * N])
+        load_y(4, 2, rest[:, 4 * N : 6 * N])
+        load_x(6, 2, rest[:, 6 * N : 8 * N])
+        load_y(6, 2, rest[:, 8 * N : 10 * N])
         nc.vector.quantize_mx(w1_codes[:].bitcast(E4M3), w1_scales[:], w_by_d[:].rearrange("p s q t -> p (s q t)"))
         prepare_x(0, nc.scalar.copy)
         score(0, ("label0", "label1"))
         prepare_x(1, nc.vector.tensor_copy)
-        turn_w(1, "score2", ring, "x2")
+        prepare_x(2, nc.vector.tensor_copy)
         for c, tiles in enumerate(CHUNKS):
             if c + 1 < len(CHUNKS):
-                score(c + 1, ("score%d" % ((2 * c) % 3), "score%d" % ((2 * c + 1) % 3)))
+                score(c + 1, ("score0", "score1"))
+            if c == 0:
+                turn_w(1, "grad2", ring, "x3")
             diffs = [weigh(k) for k in tiles]
-            if c + 1 < len(CHUNKS):
+            if 0 < c < len(CHUNKS) - 1:
                 for k in CHUNKS[c + 1]:
                     turn_y(k)
-            if c + 2 < len(CHUNKS):
-                prepare_x(c + 2, nc.scalar.copy if c else nc.vector.tensor_copy)
+            if 0 < c and c + 2 < len(CHUNKS):
+                prepare_x(c + 2, nc.scalar.copy)
+            if c > 0:
+                for k in CHUNKS[c - 1]:
+                    store(k, nc.scalar.copy, 1)
             for k, diff in zip(tiles, diffs):
                 scale(k, diff)
-            for k in tiles:
                 gradient(k)
-            for k in tiles:
-                last = k == TILES - 1
-                store(k, nc.vector.tensor_copy if last else nc.scalar.copy, 2 if last else 1)
+        store(TILES - 1, nc.vector.tensor_copy, 2)

@@ -24,7 +24,7 @@ PACK = 4
 TILES = R // P
 HALF = R // 2
 CHUNKS = [(0,), (1,), (2, 3), (4, 5), (6,), (7,)]
-LABEL_BANKS = ["label2", "grad1", "label0", "label1", "label2", "label0", "label1", "label2"]
+LABEL_BANKS = ["label2", "label0", "label1", "label2", "label0", "label1", "label2", "label0"]
 CAST_TAGS = ["x0", "x0", "x0", "x1", "x0", "x2"]
 CODE_TAGS = ["x2", "x3", "x1", "x0", "x1", "x3"]
 
@@ -66,11 +66,10 @@ def tile_attend_gsig_x_ts_kernel(tc, xT, wT, y, wt, ts, offs, out):
             for j in range(count):
                 y_raw[k + j] = view[:, j, :]
 
-        first_y = keep.tile([P, 2 * N], F32, name="first_y")
+        first_y = keep.tile([P, N], F32, name="first_y")
         for t in range(1, PACK):
             nc.sync.dma_start(planes[t][:], w_rows[:, t, :])
-        load_y(0, 1, first_y[:, 0:N])
-        load_y(1, 1, first_y[:, N : 2 * N])
+        load_y(0, 1, first_y[:])
 
         ident = keep.tile([P, P], F32, name="ident")
         make_identity(nc, ident[:])
@@ -209,11 +208,11 @@ def tile_attend_gsig_x_ts_kernel(tc, xT, wT, y, wt, ts, offs, out):
         load_x(0, 1, first_x[:])
         gather(2)
         make_factor(1)
-        second = keep.tile([P, 3 * N], F32, name="second", tag="stage2", align_bytes=64)
+        second = keep.tile([P, 4 * N], F32, name="second", tag="stage2", align_bytes=64)
         load_x(1, 1, second[:, 0:N])
+        load_y(1, 1, second[:, 3 * N : 4 * N])
         load_x(2, 2, second[:, N : 3 * N])
         turn_y(0)
-        turn_y(1)
         gather(3)
         rest = keep.tile([P, 10 * N], F32, name="rest", tag="stage3", align_bytes=64)
         load_y(2, 2, rest[:, 0 : 2 * N])
@@ -224,7 +223,7 @@ def tile_attend_gsig_x_ts_kernel(tc, xT, wT, y, wt, ts, offs, out):
         nc.vector.quantize_mx(w1_codes[:].bitcast(E4M3), w1_scales[:], w_by_d[:].rearrange("p s q t -> p (s q t)"))
         prepare_x(0, nc.scalar.copy)
         score(0, ("label0", "label1"))
-        prepare_x(1, nc.vector.tensor_copy)
+        prepare_x(1, nc.scalar.copy)
         prepare_x(2, nc.vector.tensor_copy)
         for c, tiles in enumerate(CHUNKS):
             if c + 1 < len(CHUNKS):
@@ -232,15 +231,17 @@ def tile_attend_gsig_x_ts_kernel(tc, xT, wT, y, wt, ts, offs, out):
             if c == 0:
                 turn_w(1, "grad2", ring, "x3")
             diffs = [weigh(k) for k in tiles]
-            if 0 < c < len(CHUNKS) - 1:
+            if c + 1 < len(CHUNKS):
                 for k in CHUNKS[c + 1]:
                     turn_y(k)
             if 0 < c and c + 2 < len(CHUNKS):
                 prepare_x(c + 2, nc.scalar.copy)
             if c > 0:
                 for k in CHUNKS[c - 1]:
-                    store(k, nc.scalar.copy, 1)
+                    if k < TILES - 2:
+                        store(k, nc.scalar.copy, 1)
             for k, diff in zip(tiles, diffs):
                 scale(k, diff)
                 gradient(k)
-        store(TILES - 1, nc.vector.tensor_copy, 2)
+        store(TILES - 2, nc.vector.tensor_copy, 1)
+        store(TILES - 1, nc.scalar.copy, 2)

@@ -210,12 +210,13 @@ def tile_attend_gsig_x_ts_kernel(tc, xT, wT, y, wt, ts, offs, out):
         make_factor(1)
         second = keep.tile([P, 4 * N], F32, name="second", tag="stage2", align_bytes=64)
         load_x(1, 1, second[:, 0:N])
-        load_y(1, 1, second[:, 3 * N : 4 * N])
         load_x(2, 2, second[:, N : 3 * N])
+        load_y(1, 1, second[:, 3 * N : 4 * N])
         turn_y(0)
         gather(3)
         rest = keep.tile([P, 10 * N], F32, name="rest", tag="stage3", align_bytes=64)
-        load_y(2, 2, rest[:, 0 : 2 * N])
+        load_y(2, 1, rest[:, 0:N])
+        load_y(3, 1, rest[:, N : 2 * N])
         load_x(4, 2, rest[:, 2 * N : 4 * N])
         load_y(4, 2, rest[:, 4 * N : 6 * N])
         load_x(6, 2, rest[:, 6 * N : 8 * N])

@@ -24,6 +24,7 @@ PACK = 4
 TILES = R // P
 HALF = R // 2
 CHUNKS = [(0,), (1,), (2, 3), (4, 5), (6,), (7,)]
+DEALT = (3, 5, 7)
 LABEL_BANKS = ["label2", "label0", "label1", "label2", "label0", "label1", "label2", "label0"]
 CAST_TAGS = ["x0", "x0", "x0", "x1", "x0", "x2"]
 CODE_TAGS = ["x2", "x3", "x1", "x0", "x1", "x3"]
@@ -158,8 +159,16 @@ def tile_attend_gsig_x_ts_kernel(tc, xT, wT, y, wt, ts, offs, out):
 
         def turn_y(k):
             labels[k] = psum.tile([P, PACK, P], F32, name="labels", tag=LABEL_BANKS[k])
+            columns = [y_raw[k][:, s::PACK] for s in range(PACK)]
+            if k in DEALT:
+                dealt = ring.tile([P, PACK, P], F32, name="dealt", bufs=2)
+                nc.vector.tensor_copy(
+                    dealt[:].rearrange("p s (c i) -> p c s i", i=4),
+                    y_raw[k].rearrange("p (c i s) -> p c s i", i=4, s=PACK),
+                )
+                columns = [dealt[:, s, :] for s in range(PACK)]
             for s in range(PACK):
-                nc.tensor.transpose(labels[k][:, s, :], y_raw[k][:, s::PACK], ident[:])
+                nc.tensor.transpose(labels[k][:, s, :], columns[s], ident[:])
 
         def weigh(k):
             diff = ring.tile([P, PACK, P], F32, name="diff", bufs=3)
@@ -218,9 +227,11 @@ def tile_attend_gsig_x_ts_kernel(tc, xT, wT, y, wt, ts, offs, out):
         load_y(2, 1, rest[:, 0:N])
         load_y(3, 1, rest[:, N : 2 * N])
         load_x(4, 2, rest[:, 2 * N : 4 * N])
-        load_y(4, 2, rest[:, 4 * N : 6 * N])
+        load_y(4, 1, rest[:, 4 * N : 5 * N])
+        load_y(5, 1, rest[:, 5 * N : 6 * N])
         load_x(6, 2, rest[:, 6 * N : 8 * N])
-        load_y(6, 2, rest[:, 8 * N : 10 * N])
+        load_y(6, 1, rest[:, 8 * N : 9 * N])
+        load_y(7, 1, rest[:, 9 * N : 10 * N])
         nc.vector.quantize_mx(w1_codes[:].bitcast(E4M3), w1_scales[:], w_by_d[:].rearrange("p s q t -> p (s q t)"))
         prepare_x(0, nc.scalar.copy)
         score(0, ("label0", "label1"))

@@ -23,11 +23,14 @@ P = 128
 PACK = 4
 TILES = R // P
 HALF = R // 2
-CHUNKS = [(0,), (1,), (2, 3), (4, 5), (6,), (7,)]
+CHUNKS = [(0,), (1,), (2, 3), (4, 5), (6, 7)]
 DEALT = (3, 5, 7)
-LABEL_BANKS = ["label2", "label0", "label1", "label2", "label0", "label1", "label2", "label0"]
-CAST_TAGS = ["x0", "x0", "x0", "x1", "x0", "x2"]
-CODE_TAGS = ["x2", "x3", "x1", "x0", "x1", "x3"]
+LABEL_BANKS = ["label2", "label1", "label0"]
+GRAD_BANKS = ["grad0", "grad1", "grad2", "grad0", "grad1", "grad2", "score0", "score1"]
+PROB_TAGS = ["p1", "p2", "p0", "p1", "p0"]
+CAST_TAGS = ["", "x1", "x2", "x0", "x3"]
+CODE_TAGS = ["x2", "x3", "x0", "x1", "x2"]
+DEAL_TAGS = {3: "p2", 5: "p0", 7: "p1"}
 
 
 def tile_attend_gsig_x_ts_kernel(tc, xT, wT, y, wt, ts, offs, out):
@@ -35,6 +38,7 @@ def tile_attend_gsig_x_ts_kernel(tc, xT, wT, y, wt, ts, offs, out):
     with ExitStack() as ctx:
         keep = ctx.enter_context(tc.tile_pool(name="keep", bufs=1))
         ring = ctx.enter_context(tc.tile_pool(name="ring", bufs=3))
+        shared = ctx.enter_context(tc.tile_pool(name="shared", bufs=1))
         psum = ctx.enter_context(tc.psum_pool(name="psum", bufs=1))
 
         offsets = keep.tile([P, N // 16], U16, name="offsets")
@@ -67,10 +71,8 @@ def tile_attend_gsig_x_ts_kernel(tc, xT, wT, y, wt, ts, offs, out):
             for j in range(count):
                 y_raw[k + j] = view[:, j, :]
 
-        first_y = keep.tile([P, N], F32, name="first_y")
         for t in range(1, PACK):
             nc.sync.dma_start(planes[t][:], w_rows[:, t, :])
-        load_y(0, 1, first_y[:])
 
         ident = keep.tile([P, P], F32, name="ident")
         make_identity(nc, ident[:])
@@ -91,96 +93,114 @@ def tile_attend_gsig_x_ts_kernel(tc, xT, wT, y, wt, ts, offs, out):
 
         ts_all = keep.tile([P, N], F32, name="ts_all")
         nc.vector.tensor_copy(ts_all[:], ts_window[:].indirect(offsets[:]))
-        ts_turned = psum.tile([P, PACK, P], F32, name="ts_turned", tag="label2")
+        ts_col = []
         for s in range(PACK):
-            nc.tensor.transpose(ts_turned[:, s, :], ts_all[:, s::PACK], ident[:])
-        ts_col = keep.tile([P, PACK], F32, name="ts_col")
-        nc.scalar.copy(ts_col[:], ts_turned[:, :, 0])
+            ts_turned = psum.tile([P, P], F32, name="ts_turned", tag=("grad0", "grad1", "grad2", "score1")[s])
+            nc.tensor.transpose(ts_turned[:], ts_all[:, s::PACK], ident[:])
+            ts_col.append(keep.tile([P, 1], F32, name="ts_col%d" % s))
+            nc.scalar.copy(ts_col[s][:], ts_turned[:, 0:1])
 
         factor = [keep.tile([P, PACK, HALF], F32, name="factor%d" % h) for h in range(2)]
 
         w_by_d = keep.tile([P, PACK, P, PACK], BF16, name="w_by_d", align_bytes=64)
         w_words = w_by_d[:].rearrange("p s q t -> p (s q t)").bitcast(F32).rearrange("p (s q u) -> p s q u", s=PACK, u=2)
 
-        def make_factor(h):
-            rows = neg_wt[h][:]
-            for s in range(PACK):
-                nc.scalar.activation(factor[h][:, s, :], rows, COPY, scale=ts_col[:, s : s + 1])
+        def make_factor(h, places):
+            for s in places:
+                nc.scalar.activation(factor[h][:, s, :], neg_wt[h][:], COPY, scale=ts_col[s][:])
+
+        w1_codes = keep.tile([P, N], U32, name="w1_codes", align_bytes=64)
+        w2_codes = keep.tile([P, D], U32, name="w2_codes", align_bytes=64)
+        w_by_slot, w1_scales, w2_scales = {}, {}, {}
 
         def turn_w(u, bank, pool, stage):
             w_turned = psum.tile([P, PACK, P], F32, name="w_turned", tag=bank)
             for s in range(PACK):
                 nc.tensor.transpose(w_turned[:, s, :], w_words[:, s, :, u], ident[:])
             halves = w_turned[:].rearrange("q s p -> q (s p)").bitcast(BF16)
-            w_by_slot = pool.tile([P, P, 2, PACK], BF16, name="w_by_slot", tag=stage, align_bytes=64, bufs=1)
-            nc.scalar.copy(w_by_slot[:], halves.rearrange("q (s p e) -> q p e s", s=PACK, e=2))
+            w_by_slot[u] = pool.tile([P, P, 2, PACK], BF16, name="w_by_slot", tag=stage, align_bytes=64, bufs=1)
+            nc.scalar.copy(w_by_slot[u][:], halves.rearrange("q (s p e) -> q p e s", s=PACK, e=2))
+
+        def quantize_w2(u):
             cols = slice(u * D // 2, (u + 1) * D // 2)
+            if u == 0:
+                w2_scales[0] = shared.tile([P, D], U8, name="w2_scales", align_bytes=64, offset=N)
             nc.vector.quantize_mx(
-                w2_codes[:, cols].bitcast(E4M3), w2_scales[:, cols], w_by_slot[:].rearrange("q p e s -> q (p e s)")
+                w2_codes[:, cols].bitcast(E4M3), w2_scales[0][:, cols], w_by_slot[u][:].rearrange("q p e s -> q (p e s)")
             )
 
-        w1_codes = keep.tile([P, N], U32, name="w1_codes", align_bytes=64)
-        w1_scales = keep.tile([P, N], U8, name="w1_scales", align_bytes=64)
-        w2_codes = keep.tile([P, D], U32, name="w2_codes", align_bytes=64)
-        w2_scales = keep.tile([P, D], U8, name="w2_scales", align_bytes=64)
+        def quantize_w1(half):
+            cols = slice(half * N // 2, (half + 1) * N // 2)
+            w1_scales[half] = shared.tile([P, N // 2], U8, name="w1_scales%d" % half, align_bytes=64, offset=half * N // 2)
+            nc.vector.quantize_mx(
+                w1_codes[:, cols].bitcast(E4M3), w1_scales[half][:],
+                w_by_d[:, 2 * half : 2 * half + 2, :, :].rearrange("p s q t -> p (s q t)"),
+            )
 
-        x_mx, probs, labels, h_bf, grads = {}, {}, {}, {}, {}
+        x_bf, x_mx, probs, columns, labels, diffs, h_bf, grads = {}, {}, {}, {}, {}, {}, {}, {}
 
-        def prepare_x(c, copy):
+        def cast_x(c, copy):
             width = len(CHUNKS[c]) * P
-            x_bf = ring.tile([P, width, PACK], BF16, name="x_bf", tag=CAST_TAGS[c], align_bytes=64, bufs=1)
+            if c == 0:
+                x_bf[c] = shared.tile([P, P, PACK], BF16, name="x_first", align_bytes=64, offset=0)
+            else:
+                x_bf[c] = ring.tile([P, width, PACK], BF16, name="x_bf", tag=CAST_TAGS[c], align_bytes=64, bufs=1)
             copy(
-                x_bf[:].rearrange("p (c i) t -> p c t i", i=4),
+                x_bf[c][:].rearrange("p (c i) t -> p c t i", i=4),
                 x_raw[c].rearrange("p t (c i) -> p c t i", i=4),
             )
+
+        def quantize_x(c):
+            width = len(CHUNKS[c]) * P
             x_codes = ring.tile([P, width], U32, name="x_codes", tag=CODE_TAGS[c], align_bytes=64, bufs=1)
             x_scales = ring.tile([P, width], U8, name="x_scales", align_bytes=64)
-            nc.vector.quantize_mx(x_codes[:].bitcast(E4M3), x_scales[:], x_bf[:].rearrange("p r t -> p (r t)"))
+            nc.vector.quantize_mx(x_codes[:].bitcast(E4M3), x_scales[:], x_bf[c][:].rearrange("p r t -> p (r t)"))
             x_mx[c] = (x_codes, x_scales)
 
         def score(c, banks):
             x_codes, x_scales = x_mx[c]
             width = len(CHUNKS[c]) * P
             share = PACK // len(banks)
-            chunk_probs = ring.tile([P, PACK, width], F32, name="probs", bufs=2)
+            chunk = ring.tile([P, PACK, width], F32, name="probs", tag=PROB_TAGS[c], align_bytes=64, bufs=1)
             for b, bank in enumerate(banks):
                 scores = psum.tile([P, share, width], F32, name="scores", tag=bank)
                 for e in range(share):
-                    cols = slice((share * b + e) * P, (share * b + e + 1) * P)
+                    s = share * b + e
                     nc.tensor.matmul_mx(
-                        scores[:, e, :], w1_codes[:, cols].bitcast(E4M3), w1_scales[:, cols],
+                        scores[:, e, :], w1_codes[:, s * P : (s + 1) * P].bitcast(E4M3),
+                        w1_scales[s // 2][:, s % 2 * P : (s % 2 + 1) * P],
                         x_codes[:].bitcast(E4M3), x_scales[:], start=True, stop=True,
                     )
                 for e in range(share):
                     s = share * b + e
-                    nc.scalar.activation(chunk_probs[:, s, :], scores[:, e, :], SIGMOID, scale=ts_col[:, s : s + 1])
+                    nc.scalar.activation(chunk[:, s, :], scores[:, e, :], SIGMOID, scale=ts_col[s][:])
             for j, k in enumerate(CHUNKS[c]):
-                probs[k] = chunk_probs[:, :, j * P : (j + 1) * P]
+                probs[k] = chunk[:, :, j * P : (j + 1) * P]
+
+        def deal_y(k, copy, dealt):
+            copy(
+                dealt.rearrange("p s (c i) -> p c s i", i=4),
+                y_raw[k].rearrange("p (c i s) -> p c s i", i=4, s=PACK),
+            )
+            columns[k] = [dealt[:, s, :] for s in range(PACK)]
 
         def turn_y(k):
-            labels[k] = psum.tile([P, PACK, P], F32, name="labels", tag=LABEL_BANKS[k])
-            columns = [y_raw[k][:, s::PACK] for s in range(PACK)]
-            if k in DEALT:
-                dealt = ring.tile([P, PACK, P], F32, name="dealt", bufs=2)
-                nc.vector.tensor_copy(
-                    dealt[:].rearrange("p s (c i) -> p c s i", i=4),
-                    y_raw[k].rearrange("p (c i s) -> p c s i", i=4, s=PACK),
-                )
-                columns = [dealt[:, s, :] for s in range(PACK)]
+            labels[k] = psum.tile([P, PACK, P], F32, name="labels", tag=LABEL_BANKS[k % 3])
             for s in range(PACK):
-                nc.tensor.transpose(labels[k][:, s, :], columns[s], ident[:])
+                column = columns[k][s] if k in columns else y_raw[k][:, s::PACK]
+                nc.tensor.transpose(labels[k][:, s, :], column, ident[:])
 
         def weigh(k):
-            diff = ring.tile([P, PACK, P], F32, name="diff", bufs=3)
-            nc.vector.scalar_tensor_tensor(diff[:], labels[k][:], 0.0, probs[k], MAX, SUB)
-            return diff
+            diffs[k] = ring.tile([P, PACK, P], F32, name="diff", bufs=3)
+            nc.vector.scalar_tensor_tensor(diffs[k][:], labels[k][:], 0.0, probs[k], MAX, SUB)
 
-        def scale(k, diff):
-            rows = slice(k % 4 * P, (k % 4 + 1) * P)
-            h_bf[k] = ring.tile([P, P, PACK], BF16, name="h_bf", align_bytes=64, bufs=3)
+        def scale(k, first, count):
+            rows = slice(k % 4 * P + first, k % 4 * P + first + count)
+            if first == 0:
+                h_bf[k] = ring.tile([P, P, PACK], BF16, name="h_bf", align_bytes=64, bufs=3)
             nc.vector.tensor_tensor(
-                h_bf[k][:].rearrange("q (c i) s -> q c s i", i=4),
-                diff[:].rearrange("q s (c i) -> q c s i", i=4),
+                h_bf[k][:, first : first + count, :].rearrange("q (c i) s -> q c s i", i=4),
+                diffs[k][:, :, first : first + count].rearrange("q s (c i) -> q c s i", i=4),
                 factor[k // 4][:, :, rows].rearrange("q s (c i) -> q c s i", i=4),
                 MULT,
             )
@@ -189,9 +209,9 @@ def tile_attend_gsig_x_ts_kernel(tc, xT, wT, y, wt, ts, offs, out):
             h_codes = ring.tile([P, P], U32, name="h_codes", align_bytes=64)
             h_scales = ring.tile([P, P], U8, name="h_scales", align_bytes=64)
             nc.vector.quantize_mx(h_codes[:].bitcast(E5M2), h_scales[:], h_bf[k][:].rearrange("q r s -> q (r s)"))
-            grads[k] = psum.tile([P, D], F32, name="grad", tag="grad%d" % (k % 3))
+            grads[k] = psum.tile([P, D], F32, name="grad", tag=GRAD_BANKS[k])
             nc.tensor.matmul_mx(
-                grads[k][:], h_codes[:].bitcast(E5M2), h_scales[:], w2_codes[:].bitcast(E4M3), w2_scales[:],
+                grads[k][:], h_codes[:].bitcast(E5M2), h_scales[:], w2_codes[:].bitcast(E4M3), w2_scales[0][:],
                 start=True, stop=True,
             )
 
@@ -210,13 +230,16 @@ def tile_attend_gsig_x_ts_kernel(tc, xT, wT, y, wt, ts, offs, out):
             nc.vector.tensor_copy(w_by_d[:, :, :, t].rearrange("p s q -> p q s"), planes[t][:].indirect(offsets[:]))
 
         gather(0)
-        make_factor(0)
+        for s in range(2):
+            nc.vector.tensor_scalar(factor[1][:, s, :], neg_wt[1][:], ts_col[s][:], None, MULT)
+        make_factor(0, range(PACK))
         gather(1)
         turn_w(0, "score0", keep, "wt0")
-        first_x = keep.tile([P, N], F32, name="first_x", tag="stage1", align_bytes=64)
-        load_x(0, 1, first_x[:])
+        first = keep.tile([P, 2 * N], F32, name="first", tag="stage1", align_bytes=64)
+        load_x(0, 1, first[:, 0:N])
+        load_y(0, 1, first[:, N : 2 * N])
         gather(2)
-        make_factor(1)
+        make_factor(1, range(2, PACK))
         second = keep.tile([P, 4 * N], F32, name="second", tag="stage2", align_bytes=64)
         load_x(1, 1, second[:, 0:N])
         load_x(2, 2, second[:, N : 3 * N])
@@ -225,35 +248,56 @@ def tile_attend_gsig_x_ts_kernel(tc, xT, wT, y, wt, ts, offs, out):
         gather(3)
         rest = keep.tile([P, 10 * N], F32, name="rest", tag="stage3", align_bytes=64)
         load_y(2, 1, rest[:, 0:N])
-        load_y(3, 1, rest[:, N : 2 * N])
         load_x(4, 2, rest[:, 2 * N : 4 * N])
+        load_y(3, 1, rest[:, N : 2 * N])
         load_y(4, 1, rest[:, 4 * N : 5 * N])
-        load_y(5, 1, rest[:, 5 * N : 6 * N])
         load_x(6, 2, rest[:, 6 * N : 8 * N])
+        load_y(5, 1, rest[:, 5 * N : 6 * N])
         load_y(6, 1, rest[:, 8 * N : 9 * N])
         load_y(7, 1, rest[:, 9 * N : 10 * N])
-        nc.vector.quantize_mx(w1_codes[:].bitcast(E4M3), w1_scales[:], w_by_d[:].rearrange("p s q t -> p (s q t)"))
-        prepare_x(0, nc.scalar.copy)
+        cast_x(0, nc.scalar.copy)
+        quantize_x(0)
+        quantize_w1(0)
+        quantize_w1(1)
+        quantize_w2(0)
+        cast_x(1, nc.scalar.copy)
         score(0, ("label0", "label1"))
-        prepare_x(1, nc.scalar.copy)
-        prepare_x(2, nc.vector.tensor_copy)
-        for c, tiles in enumerate(CHUNKS):
-            if c + 1 < len(CHUNKS):
-                score(c + 1, ("score0", "score1"))
-            if c == 0:
-                turn_w(1, "grad2", ring, "x3")
-            diffs = [weigh(k) for k in tiles]
-            if c + 1 < len(CHUNKS):
-                for k in CHUNKS[c + 1]:
-                    turn_y(k)
-            if 0 < c and c + 2 < len(CHUNKS):
-                prepare_x(c + 2, nc.scalar.copy)
-            if c > 0:
-                for k in CHUNKS[c - 1]:
-                    if k < TILES - 2:
-                        store(k, nc.scalar.copy, 1)
-            for k, diff in zip(tiles, diffs):
-                scale(k, diff)
-                gradient(k)
-        store(TILES - 2, nc.vector.tensor_copy, 1)
+        quantize_x(1)
+        cast_x(2, nc.vector.tensor_copy)
+        quantize_x(2)
+        score(1, ("grad2",))
+        turn_w(1, "label0", ring, "x3")
+        turn_y(1)
+        score(2, ("score0", "score1"))
+        cast_x(3, nc.scalar.copy)
+        for k in range(TILES - 1):
+            c = k // 2 + 3
+            weigh(k)
+            if k == 1:
+                quantize_w2(1)
+                cast_x(4, nc.scalar.copy)
+            if k > 0:
+                gradient(k - 1)
+            if k + 2 < TILES:
+                if k + 2 in DEALT:
+                    dealt = ring.tile([P, PACK, P], F32, name="dealt", tag=DEAL_TAGS[k + 2], align_bytes=64, bufs=1)
+                    deal_y(k + 2, nc.vector.tensor_copy, dealt[:])
+                turn_y(k + 2)
+            if k % 2 == 1 and c < len(CHUNKS):
+                quantize_x(c)
+            if k == 1:
+                score(3, ("score0", "score1"))
+            if k > 1:
+                store(k - 2, nc.scalar.copy, 1)
+            if k == 4:
+                score(4, ("score0", "score1"))
+            if k == TILES - 2:
+                weigh(k + 1)
+            scale(k, 0, P)
+        scale(TILES - 1, 0, P // 2)
+        gradient(TILES - 2)
+        store(TILES - 3, nc.scalar.copy, 1)
+        scale(TILES - 1, P // 2, P // 2)
+        gradient(TILES - 1)
+        store(TILES - 2, nc.scalar.copy, 1)
         store(TILES - 1, nc.scalar.copy, 2)

@@ -24,13 +24,13 @@ PACK = 4
 TILES = R // P
 HALF = R // 2
 CHUNKS = [(0,), (1,), (2, 3), (4, 5), (6, 7)]
-DEALT = (3, 5, 7)
+DEALT = (3, 5)
 LABEL_BANKS = ["label2", "label1", "label0"]
 GRAD_BANKS = ["grad0", "grad1", "grad2", "grad0", "grad1", "grad2", "score0", "score1"]
 PROB_TAGS = ["p1", "p2", "p0", "p1", "p0"]
-CAST_TAGS = ["", "x1", "x2", "x0", "x3"]
+CAST_TAGS = ["", "x1", "x2", "x0"]
 CODE_TAGS = ["x2", "x3", "x0", "x1", "x2"]
-DEAL_TAGS = {3: "p2", 5: "p0", 7: "p1"}
+DEAL_TAGS = {3: "p2", 5: "p0"}
 
 
 def tile_attend_gsig_x_ts_kernel(tc, xT, wT, y, wt, ts, offs, out):
@@ -39,17 +39,18 @@ def tile_attend_gsig_x_ts_kernel(tc, xT, wT, y, wt, ts, offs, out):
         keep = ctx.enter_context(tc.tile_pool(name="keep", bufs=1))
         ring = ctx.enter_context(tc.tile_pool(name="ring", bufs=3))
         shared = ctx.enter_context(tc.tile_pool(name="shared", bufs=1))
+        late = ctx.enter_context(tc.tile_pool(name="late", bufs=1))
         psum = ctx.enter_context(tc.psum_pool(name="psum", bufs=1))
 
         offsets = keep.tile([P, N // 16], U16, name="offsets")
         w_rows = wT.rearrange("(p t) c -> p t c", t=PACK)
-        planes = [keep.tile([P, T], F32, name="plane%d" % t, tag="stage%d" % t, align_bytes=64) for t in range(PACK)]
-        ts_window = keep.tile([P, T], F32, name="ts_window")
+        planes = [keep.tile([P, T], F32, name="plane%d" % t, tag="stage%d" % t, align_bytes=64) for t in range(PACK - 1)]
+        ts_window = late.tile([P, T], F32, name="ts_window", align_bytes=64, offset=0)
         wt_runs = keep.tile([P, TILES], F32, name="wt_runs")
         nc.vector.memset(ts_window[:, 0 : T // 2], 0.0)
         nc.gpsimd.memset(ts_window[:, T // 2 : T], 0.0)
-        nc.sync.dma_start(wt_runs[:], wt[0].rearrange("(n m) o -> n (m o)", n=P))
         nc.sync.dma_start(planes[0][:, 0 : T // 2], w_rows[:, 0, 0 : T // 2])
+        nc.sync.dma_start(wt_runs[:], wt[0].rearrange("(n m) o -> n (m o)", n=P))
         nc.sync.dma_start(offsets[:], offs)
         nc.sync.dma_start(ts_window[0:1, 0 : T // 2], ts[0:1, 0 : T // 2])
         nc.sync.dma_start(ts_window[0:1, T // 2 : T], ts[0:1, T // 2 : T])
@@ -71,11 +72,13 @@ def tile_attend_gsig_x_ts_kernel(tc, xT, wT, y, wt, ts, offs, out):
             for j in range(count):
                 y_raw[k + j] = view[:, j, :]
 
-        for t in range(1, PACK):
+        for t in range(1, PACK - 1):
             nc.sync.dma_start(planes[t][:], w_rows[:, t, :])
 
         ident = keep.tile([P, P], F32, name="ident")
         make_identity(nc, ident[:])
+        ident_bf = keep.tile([P, P], BF16, name="ident_bf")
+        make_identity(nc, ident_bf[:])
         warm = keep.tile([P, 1], F32, name="warm")
         nc.scalar.activation(warm[:], ident[:, 0:1], SIGMOID)
 
@@ -93,6 +96,8 @@ def tile_attend_gsig_x_ts_kernel(tc, xT, wT, y, wt, ts, offs, out):
 
         ts_all = keep.tile([P, N], F32, name="ts_all")
         nc.vector.tensor_copy(ts_all[:], ts_window[:].indirect(offsets[:]))
+        planes.append(late.tile([P, T], F32, name="plane3", align_bytes=64, offset=0))
+        nc.sync.dma_start(planes[PACK - 1][:], w_rows[:, PACK - 1, :])
         ts_col = []
         for s in range(PACK):
             ts_turned = psum.tile([P, P], F32, name="ts_turned", tag=("grad0", "grad1", "grad2", "score1")[s])
@@ -111,22 +116,29 @@ def tile_attend_gsig_x_ts_kernel(tc, xT, wT, y, wt, ts, offs, out):
 
         w1_codes = keep.tile([P, N], U32, name="w1_codes", align_bytes=64)
         w2_codes = keep.tile([P, D], U32, name="w2_codes", align_bytes=64)
-        w_by_slot, w1_scales, w2_scales = {}, {}, {}
+        w2_scales = keep.tile([P, D], U8, name="w2_scales", align_bytes=64)
+        w_by_slot, w1_scales = {}, {}
 
-        def turn_w(u, bank, pool, stage):
+        def turn_words(bank):
             w_turned = psum.tile([P, PACK, P], F32, name="w_turned", tag=bank)
             for s in range(PACK):
-                nc.tensor.transpose(w_turned[:, s, :], w_words[:, s, :, u], ident[:])
+                nc.tensor.transpose(w_turned[:, s, :], w_words[:, s, :, 0], ident[:])
             halves = w_turned[:].rearrange("q s p -> q (s p)").bitcast(BF16)
-            w_by_slot[u] = pool.tile([P, P, 2, PACK], BF16, name="w_by_slot", tag=stage, align_bytes=64, bufs=1)
-            nc.scalar.copy(w_by_slot[u][:], halves.rearrange("q (s p e) -> q p e s", s=PACK, e=2))
+            w_by_slot[0] = keep.tile([P, 2, P, PACK], BF16, name="w_by_slot", tag="wt0", align_bytes=64)
+            nc.scalar.copy(w_by_slot[0][:], halves.rearrange("q (s p e) -> q e p s", s=PACK, e=2))
+
+        def turn_plane(t, bank):
+            w_turned = psum.tile([P, PACK, P], BF16, name="plane_turned", tag=bank)
+            for s in range(PACK):
+                nc.tensor.transpose(w_turned[:, s, :], w_by_d[:, s, :, t], ident_bf[:])
+            if t == 2:
+                w_by_slot[1] = keep.tile([P, 2, P, PACK], BF16, name="w_by_slot", tag="wt1", align_bytes=64)
+            nc.scalar.copy(w_by_slot[1][:, t - 2, :, :], w_turned[:].rearrange("q s p -> q p s"))
 
         def quantize_w2(u):
             cols = slice(u * D // 2, (u + 1) * D // 2)
-            if u == 0:
-                w2_scales[0] = shared.tile([P, D], U8, name="w2_scales", align_bytes=64, offset=N)
             nc.vector.quantize_mx(
-                w2_codes[:, cols].bitcast(E4M3), w2_scales[0][:, cols], w_by_slot[u][:].rearrange("q p e s -> q (p e s)")
+                w2_codes[:, cols].bitcast(E4M3), w2_scales[:, cols], w_by_slot[u][:].rearrange("q e p s -> q (e p s)")
             )
 
         def quantize_w1(half):
@@ -143,6 +155,8 @@ def tile_attend_gsig_x_ts_kernel(tc, xT, wT, y, wt, ts, offs, out):
             width = len(CHUNKS[c]) * P
             if c == 0:
                 x_bf[c] = shared.tile([P, P, PACK], BF16, name="x_first", align_bytes=64, offset=0)
+            elif c == len(CHUNKS) - 1:
+                x_bf[c] = keep.tile([P, width, PACK], BF16, name="x_last", tag="wt1", align_bytes=64)
             else:
                 x_bf[c] = ring.tile([P, width, PACK], BF16, name="x_bf", tag=CAST_TAGS[c], align_bytes=64, bufs=1)
             copy(
@@ -152,8 +166,12 @@ def tile_attend_gsig_x_ts_kernel(tc, xT, wT, y, wt, ts, offs, out):
 
         def quantize_x(c):
             width = len(CHUNKS[c]) * P
-            x_codes = ring.tile([P, width], U32, name="x_codes", tag=CODE_TAGS[c], align_bytes=64, bufs=1)
-            x_scales = ring.tile([P, width], U8, name="x_scales", align_bytes=64)
+            if c == 0:
+                x_codes = late.tile([P, width], U32, name="first_codes", align_bytes=64, offset=0)
+                x_scales = ring.tile([P, width], U8, name="first_scales", tag=CODE_TAGS[c], align_bytes=64, bufs=1)
+            else:
+                x_codes = ring.tile([P, width], U32, name="x_codes", tag=CODE_TAGS[c], align_bytes=64, bufs=1)
+                x_scales = ring.tile([P, width], U8, name="x_scales", align_bytes=64)
             nc.vector.quantize_mx(x_codes[:].bitcast(E4M3), x_scales[:], x_bf[c][:].rearrange("p r t -> p (r t)"))
             x_mx[c] = (x_codes, x_scales)
 
@@ -211,18 +229,18 @@ def tile_attend_gsig_x_ts_kernel(tc, xT, wT, y, wt, ts, offs, out):
             nc.vector.quantize_mx(h_codes[:].bitcast(E5M2), h_scales[:], h_bf[k][:].rearrange("q r s -> q (r s)"))
             grads[k] = psum.tile([P, D], F32, name="grad", tag=GRAD_BANKS[k])
             nc.tensor.matmul_mx(
-                grads[k][:], h_codes[:].bitcast(E5M2), h_scales[:], w2_codes[:].bitcast(E4M3), w2_scales[0][:],
+                grads[k][:], h_codes[:].bitcast(E5M2), h_scales[:], w2_codes[:].bitcast(E4M3), w2_scales[:],
                 start=True, stop=True,
             )
 
         def store(k, copy, pieces):
             result = ring.tile([P, D], F32, name="result", bufs=4)
-            ordered = grads[k][:].rearrange("r (u p e) -> r p u e", u=2, e=2)
+            ordered = grads[k][:].rearrange("r (t p) -> r p t", t=PACK)
             for piece in range(pieces):
                 cols = slice(piece * D // pieces, (piece + 1) * D // pieces)
                 copy(
-                    result[:, cols].rearrange("r (p u e) -> r p u e", u=2, e=2),
-                    ordered[:, piece * P // pieces : (piece + 1) * P // pieces, :, :],
+                    result[:, cols].rearrange("r (p t) -> r p t", t=PACK),
+                    ordered[:, piece * P // pieces : (piece + 1) * P // pieces, :],
                 )
                 nc.sync.dma_start(out[0, k * P : (k + 1) * P, cols], result[:, cols])
 
@@ -234,19 +252,21 @@ def tile_attend_gsig_x_ts_kernel(tc, xT, wT, y, wt, ts, offs, out):
             nc.vector.tensor_scalar(factor[1][:, s, :], neg_wt[1][:], ts_col[s][:], None, MULT)
         make_factor(0, range(PACK))
         gather(1)
-        turn_w(0, "score0", keep, "wt0")
+        turn_words("score0")
         first = keep.tile([P, 2 * N], F32, name="first", tag="stage1", align_bytes=64)
         load_x(0, 1, first[:, 0:N])
         load_y(0, 1, first[:, N : 2 * N])
         gather(2)
         make_factor(1, range(2, PACK))
+        turn_plane(2, "grad0")
         second = keep.tile([P, 4 * N], F32, name="second", tag="stage2", align_bytes=64)
         load_x(1, 1, second[:, 0:N])
         load_x(2, 2, second[:, N : 3 * N])
         load_y(1, 1, second[:, 3 * N : 4 * N])
         turn_y(0)
+        quantize_w2(0)
         gather(3)
-        rest = keep.tile([P, 10 * N], F32, name="rest", tag="stage3", align_bytes=64)
+        rest = late.tile([P, 10 * N], F32, name="rest", align_bytes=64, offset=N)
         load_y(2, 1, rest[:, 0:N])
         load_x(4, 2, rest[:, 2 * N : 4 * N])
         load_y(3, 1, rest[:, N : 2 * N])
@@ -259,14 +279,13 @@ def tile_attend_gsig_x_ts_kernel(tc, xT, wT, y, wt, ts, offs, out):
         quantize_x(0)
         quantize_w1(0)
         quantize_w1(1)
-        quantize_w2(0)
         cast_x(1, nc.scalar.copy)
         score(0, ("label0", "label1"))
         quantize_x(1)
         cast_x(2, nc.vector.tensor_copy)
         quantize_x(2)
         score(1, ("grad2",))
-        turn_w(1, "label0", ring, "x3")
+        turn_plane(3, "label0")
         turn_y(1)
         score(2, ("score0", "score1"))
         cast_x(3, nc.scalar.copy)

@@ -24,13 +24,7 @@ PACK = 4
 TILES = R // P
 HALF = R // 2
 CHUNKS = [(0,), (1,), (2, 3), (4, 5), (6, 7)]
-DEALT = (3, 5)
-LABEL_BANKS = ["label2", "label1", "label0"]
-GRAD_BANKS = ["grad0", "grad1", "grad2", "grad0", "grad1", "grad2", "score0", "score1"]
-PROB_TAGS = ["p1", "p2", "p0", "p1", "p0"]
-CAST_TAGS = ["", "x1", "x2", "x0"]
-CODE_TAGS = ["x2", "x3", "x0", "x1", "x2"]
-DEAL_TAGS = {3: "p2", 5: "p0"}
+KIB = 1024
 
 
 def tile_attend_gsig_x_ts_kernel(tc, xT, wT, y, wt, ts, offs, out):
@@ -40,6 +34,7 @@ def tile_attend_gsig_x_ts_kernel(tc, xT, wT, y, wt, ts, offs, out):
         ring = ctx.enter_context(tc.tile_pool(name="ring", bufs=3))
         shared = ctx.enter_context(tc.tile_pool(name="shared", bufs=1))
         late = ctx.enter_context(tc.tile_pool(name="late", bufs=1))
+        held = ctx.enter_context(tc.tile_pool(name="held", bufs=1))
         psum = ctx.enter_context(tc.psum_pool(name="psum", bufs=1))
 
         offsets = keep.tile([P, N // 16], U16, name="offsets")
@@ -82,9 +77,12 @@ def tile_attend_gsig_x_ts_kernel(tc, xT, wT, y, wt, ts, offs, out):
         warm = keep.tile([P, 1], F32, name="warm")
         nc.scalar.activation(warm[:], ident[:, 0:1], SIGMOID)
 
-        neg_wt = [keep.tile([P, HALF], F32, name="neg_wt", tag="wt%d" % h, align_bytes=64) for h in range(2)]
+        neg_wt = [
+            keep.tile([P, HALF], F32, name="neg_wt0", tag="wt0", align_bytes=64),
+            held.tile([P, HALF], F32, name="neg_wt1", align_bytes=64, offset=2 * KIB),
+        ]
         for b in range(TILES // PACK):
-            spread = psum.tile([P, PACK, P], F32, name="spread", tag="label%d" % b)
+            spread = psum.tile([P, PACK, P], F32, name="spread", tag=("label1", "grad3")[b])
             for m in range(PACK):
                 column = b * PACK + m
                 nc.tensor.transpose(spread[:, m, :], wt_runs[:, column : column + 1].to_broadcast([P, P]), ident[:])
@@ -132,7 +130,7 @@ def tile_attend_gsig_x_ts_kernel(tc, xT, wT, y, wt, ts, offs, out):
             for s in range(PACK):
                 nc.tensor.transpose(w_turned[:, s, :], w_by_d[:, s, :, t], ident_bf[:])
             if t == 2:
-                w_by_slot[1] = keep.tile([P, 2, P, PACK], BF16, name="w_by_slot", tag="wt1", align_bytes=64)
+                w_by_slot[1] = held.tile([P, 2, P, PACK], BF16, name="w_by_slot1", align_bytes=64, offset=2 * KIB)
             nc.scalar.copy(w_by_slot[1][:, t - 2, :, :], w_turned[:].rearrange("q s p -> q p s"))
 
         def quantize_w2(u):
@@ -149,37 +147,30 @@ def tile_attend_gsig_x_ts_kernel(tc, xT, wT, y, wt, ts, offs, out):
                 w_by_d[:, 2 * half : 2 * half + 2, :, :].rearrange("p s q t -> p (s q t)"),
             )
 
-        x_bf, x_mx, probs, columns, labels, diffs, h_bf, grads = {}, {}, {}, {}, {}, {}, {}, {}
+        x_bf, x_mx, probs, columns, labels, diffs, h_bf, h_mx, grads = {}, {}, {}, {}, {}, {}, {}, {}, {}
 
-        def cast_x(c, copy):
-            width = len(CHUNKS[c]) * P
-            if c == 0:
-                x_bf[c] = shared.tile([P, P, PACK], BF16, name="x_first", align_bytes=64, offset=0)
-            elif c == len(CHUNKS) - 1:
-                x_bf[c] = keep.tile([P, width, PACK], BF16, name="x_last", tag="wt1", align_bytes=64)
-            else:
-                x_bf[c] = ring.tile([P, width, PACK], BF16, name="x_bf", tag=CAST_TAGS[c], align_bytes=64, bufs=1)
+        def cast_x(c, copy, tile, first=0):
+            width = tile.shape[1]
             copy(
-                x_bf[c][:].rearrange("p (c i) t -> p c t i", i=4),
-                x_raw[c].rearrange("p t (c i) -> p c t i", i=4),
+                tile[:].rearrange("p (c i) t -> p c t i", i=4),
+                x_raw[c][:, :, first : first + width].rearrange("p t (c i) -> p c t i", i=4),
             )
+            x_bf.setdefault(c, []).append(tile)
 
-        def quantize_x(c):
-            width = len(CHUNKS[c]) * P
-            if c == 0:
-                x_codes = late.tile([P, width], U32, name="first_codes", align_bytes=64, offset=0)
-                x_scales = ring.tile([P, width], U8, name="first_scales", tag=CODE_TAGS[c], align_bytes=64, bufs=1)
-            else:
-                x_codes = ring.tile([P, width], U32, name="x_codes", tag=CODE_TAGS[c], align_bytes=64, bufs=1)
-                x_scales = ring.tile([P, width], U8, name="x_scales", align_bytes=64)
-            nc.vector.quantize_mx(x_codes[:].bitcast(E4M3), x_scales[:], x_bf[c][:].rearrange("p r t -> p (r t)"))
+        def quantize_x(c, x_codes, x_scales):
+            first = 0
+            for tile in x_bf[c]:
+                cols = slice(first, first + tile.shape[1])
+                nc.vector.quantize_mx(
+                    x_codes[:, cols].bitcast(E4M3), x_scales[:, cols], tile[:].rearrange("p r t -> p (r t)")
+                )
+                first = cols.stop
             x_mx[c] = (x_codes, x_scales)
 
-        def score(c, banks):
+        def score(c, banks, chunk):
             x_codes, x_scales = x_mx[c]
             width = len(CHUNKS[c]) * P
             share = PACK // len(banks)
-            chunk = ring.tile([P, PACK, width], F32, name="probs", tag=PROB_TAGS[c], align_bytes=64, bufs=1)
             for b, bank in enumerate(banks):
                 scores = psum.tile([P, share, width], F32, name="scores", tag=bank)
                 for e in range(share):
@@ -203,7 +194,7 @@ def tile_attend_gsig_x_ts_kernel(tc, xT, wT, y, wt, ts, offs, out):
             columns[k] = [dealt[:, s, :] for s in range(PACK)]
 
         def turn_y(k):
-            labels[k] = psum.tile([P, PACK, P], F32, name="labels", tag=LABEL_BANKS[k % 3])
+            labels[k] = psum.tile([P, PACK, P], F32, name="labels", tag="label%d" % (k % 2))
             for s in range(PACK):
                 column = columns[k][s] if k in columns else y_raw[k][:, s::PACK]
                 nc.tensor.transpose(labels[k][:, s, :], column, ident[:])
@@ -223,11 +214,15 @@ def tile_attend_gsig_x_ts_kernel(tc, xT, wT, y, wt, ts, offs, out):
                 MULT,
             )
 
-        def gradient(k):
+        def quantize_h(k):
             h_codes = ring.tile([P, P], U32, name="h_codes", align_bytes=64)
             h_scales = ring.tile([P, P], U8, name="h_scales", align_bytes=64)
             nc.vector.quantize_mx(h_codes[:].bitcast(E5M2), h_scales[:], h_bf[k][:].rearrange("q r s -> q (r s)"))
-            grads[k] = psum.tile([P, D], F32, name="grad", tag=GRAD_BANKS[k])
+            h_mx[k] = (h_codes, h_scales)
+
+        def product(k):
+            h_codes, h_scales = h_mx[k]
+            grads[k] = psum.tile([P, D], F32, name="grad", tag="grad%d" % (k % 4))
             nc.tensor.matmul_mx(
                 grads[k][:], h_codes[:].bitcast(E5M2), h_scales[:], w2_codes[:].bitcast(E4M3), w2_scales[:],
                 start=True, stop=True,
@@ -267,56 +262,83 @@ def tile_attend_gsig_x_ts_kernel(tc, xT, wT, y, wt, ts, offs, out):
         quantize_w2(0)
         gather(3)
         rest = late.tile([P, 10 * N], F32, name="rest", align_bytes=64, offset=N)
-        load_y(2, 1, rest[:, 0:N])
-        load_x(4, 2, rest[:, 2 * N : 4 * N])
-        load_y(3, 1, rest[:, N : 2 * N])
-        load_y(4, 1, rest[:, 4 * N : 5 * N])
-        load_x(6, 2, rest[:, 6 * N : 8 * N])
-        load_y(5, 1, rest[:, 5 * N : 6 * N])
-        load_y(6, 1, rest[:, 8 * N : 9 * N])
-        load_y(7, 1, rest[:, 9 * N : 10 * N])
-        cast_x(0, nc.scalar.copy)
-        quantize_x(0)
+        load_x(4, 2, rest[:, 0 : 2 * N])
+        load_y(2, 1, rest[:, 2 * N : 3 * N])
+        load_y(3, 1, rest[:, 3 * N : 4 * N])
+        load_x(6, 2, rest[:, 4 * N : 6 * N])
+        for k in range(4, TILES):
+            load_y(k, 1, rest[:, (k + 2) * N : (k + 3) * N])
+
+        def bf_tile(pool, rows, name, **place):
+            return pool.tile([P, rows, PACK], BF16, name=name, align_bytes=64, **place)
+
+        def scales_tile(rows):
+            return ring.tile([P, rows], U8, name="x_scales", align_bytes=64)
+
+        cast_x(0, nc.scalar.copy, bf_tile(shared, P, "x_first", offset=0))
+        quantize_x(
+            0, late.tile([P, P], U32, name="first_codes", align_bytes=64, offset=0),
+            keep.tile([P, P], U8, name="first_scales", tag="after_m0", align_bytes=64),
+        )
         quantize_w1(0)
         quantize_w1(1)
-        cast_x(1, nc.scalar.copy)
-        score(0, ("label0", "label1"))
-        quantize_x(1)
-        cast_x(2, nc.vector.tensor_copy)
-        quantize_x(2)
-        score(1, ("grad2",))
-        turn_plane(3, "label0")
+        cast_x(1, nc.scalar.copy, bf_tile(keep, P, "x_bf1"))
+        score(0, ("label1", "grad0"), keep.tile([P, PACK, P], F32, name="probs0", tag="after_w0", align_bytes=64))
+        quantize_x(1, keep.tile([P, P], U32, name="codes1", tag="after_m1", align_bytes=64), scales_tile(P))
+        cast_x(2, nc.vector.tensor_copy, bf_tile(keep, 2 * P, "x_bf2", tag="after_m0"))
+        score(1, ("grad1",), held.tile([P, PACK, P], F32, name="probs1", align_bytes=64, offset=6 * KIB))
         turn_y(1)
-        score(2, ("score0", "score1"))
-        cast_x(3, nc.scalar.copy)
-        for k in range(TILES - 1):
-            c = k // 2 + 3
+        weigh(0)
+        quantize_x(2, keep.tile([P, 2 * P], U32, name="codes2", tag="after_w0", align_bytes=64), scales_tile(2 * P))
+        scale(0, 0, P)
+        cast_x(3, nc.scalar.copy, bf_tile(keep, P, "x_bf3a", tag="after_m1"))
+        turn_plane(3, "label0")
+        score(2, ("score0", "score1"), keep.tile([P, PACK, 2 * P], F32, name="probs2", tag="after_w3", align_bytes=64))
+        turn_y(2)
+        weigh(1)
+        quantize_h(0)
+        cast_x(3, nc.vector.tensor_copy, bf_tile(held, P, "x_bf3b", offset=6 * KIB), P)
+        deal_y(3, nc.vector.tensor_copy, held.tile([P, PACK, P], F32, name="dealt3", align_bytes=64, offset=7 * KIB)[:])
+        quantize_w2(1)
+        product(0)
+        turn_y(3)
+        scale(1, 0, P)
+        quantize_x(3, held.tile([P, 2 * P], U32, name="codes3", align_bytes=64, offset=2 * KIB), scales_tile(2 * P))
+        cast_x(4, nc.scalar.copy, bf_tile(keep, 2 * P, "x_bf4", tag="after_w0"))
+        weigh(2)
+        score(3, ("score0", "score1"), keep.tile([P, PACK, 2 * P], F32, name="probs3", align_bytes=64))
+        quantize_h(1)
+        turn_y(4)
+        product(1)
+        scale(2, 0, P)
+        weigh(3)
+        quantize_h(2)
+        product(2)
+        quantize_x(4, keep.tile([P, 2 * P], U32, name="codes4", align_bytes=64), scales_tile(2 * P))
+        deal_y(5, nc.vector.tensor_copy, keep.tile([P, PACK, P], F32, name="dealt5", tag="after_w3", align_bytes=64)[:])
+        turn_y(5)
+        scale(3, 0, P)
+        store(0, nc.scalar.copy, 1)
+        deal_y(6, nc.scalar.copy, held.tile([P, PACK, P], F32, name="dealt6", align_bytes=64, offset=KIB // 2)[:])
+        deal_y(7, nc.scalar.copy, held.tile([P, PACK, P], F32, name="dealt7", align_bytes=64, offset=5 * KIB // 2)[:])
+        score(4, ("score0", "score1"), keep.tile([P, PACK, 2 * P], F32, name="probs4", align_bytes=64))
+        store(1, nc.scalar.copy, 1)
+        store(2, nc.scalar.copy, 1)
+        for k in (4, 5, 6):
             weigh(k)
-            if k == 1:
-                quantize_w2(1)
-                cast_x(4, nc.scalar.copy)
-            if k > 0:
-                gradient(k - 1)
+            quantize_h(k - 1)
             if k + 2 < TILES:
-                if k + 2 in DEALT:
-                    dealt = ring.tile([P, PACK, P], F32, name="dealt", tag=DEAL_TAGS[k + 2], align_bytes=64, bufs=1)
-                    deal_y(k + 2, nc.vector.tensor_copy, dealt[:])
                 turn_y(k + 2)
-            if k % 2 == 1 and c < len(CHUNKS):
-                quantize_x(c)
-            if k == 1:
-                score(3, ("score0", "score1"))
-            if k > 1:
-                store(k - 2, nc.scalar.copy, 1)
-            if k == 4:
-                score(4, ("score0", "score1"))
-            if k == TILES - 2:
-                weigh(k + 1)
+            product(k - 1)
+            store(k - 1, nc.scalar.copy, 1)
+            if k == 6:
+                weigh(7)
             scale(k, 0, P)
         scale(TILES - 1, 0, P // 2)
-        gradient(TILES - 2)
-        store(TILES - 3, nc.scalar.copy, 1)
+        quantize_h(TILES - 2)
+        product(TILES - 2)
         scale(TILES - 1, P // 2, P // 2)
-        gradient(TILES - 1)
+        quantize_h(TILES - 1)
+        product(TILES - 1)
         store(TILES - 2, nc.scalar.copy, 1)
         store(TILES - 1, nc.scalar.copy, 2)

@@ -315,12 +315,10 @@ def tile_attend_gsig_x_ts_kernel(tc, xT, wT, y, wt, ts, offs, out):
         quantize_h(2)
         product(2)
         quantize_x(4, keep.tile([P, 2 * P], U32, name="codes4", align_bytes=64), scales_tile(2 * P))
-        deal_y(5, nc.vector.tensor_copy, keep.tile([P, PACK, P], F32, name="dealt5", tag="after_w3", align_bytes=64)[:])
+        deal_y(5, nc.scalar.copy, held.tile([P, PACK, P], F32, name="dealt5", align_bytes=64, offset=KIB // 2)[:])
         turn_y(5)
         scale(3, 0, P)
         store(0, nc.scalar.copy, 1)
-        deal_y(6, nc.scalar.copy, held.tile([P, PACK, P], F32, name="dealt6", align_bytes=64, offset=KIB // 2)[:])
-        deal_y(7, nc.scalar.copy, held.tile([P, PACK, P], F32, name="dealt7", align_bytes=64, offset=5 * KIB // 2)[:])
         score(4, ("score0", "score1"), keep.tile([P, PACK, 2 * P], F32, name="probs4", align_bytes=64))
         store(1, nc.scalar.copy, 1)
         store(2, nc.scalar.copy, 1)

@@ -288,8 +288,8 @@ def tile_attend_gsig_x_ts_kernel(tc, xT, wT, y, wt, ts, offs, out):
         cast_x(2, nc.vector.tensor_copy, bf_tile(keep, 2 * P, "x_bf2", tag="after_m0"))
         score(1, ("grad1",), held.tile([P, PACK, P], F32, name="probs1", align_bytes=64, offset=6 * KIB))
         turn_y(1)
+        quantize_x(2, keep.tile([P, 2 * P], U32, name="codes2", tag="after_m2", align_bytes=64), scales_tile(2 * P))
         weigh(0)
-        quantize_x(2, keep.tile([P, 2 * P], U32, name="codes2", tag="after_w0", align_bytes=64), scales_tile(2 * P))
         scale(0, 0, P)
         cast_x(3, nc.scalar.copy, bf_tile(keep, P, "x_bf3a", tag="after_m1"))
         turn_plane(3, "label0")
@@ -304,7 +304,7 @@ def tile_attend_gsig_x_ts_kernel(tc, xT, wT, y, wt, ts, offs, out):
         turn_y(3)
         scale(1, 0, P)
         quantize_x(3, held.tile([P, 2 * P], U32, name="codes3", align_bytes=64, offset=2 * KIB), scales_tile(2 * P))
-        cast_x(4, nc.scalar.copy, bf_tile(keep, 2 * P, "x_bf4", tag="after_w0"))
+        cast_x(4, nc.scalar.copy, bf_tile(keep, 2 * P, "x_bf4", tag="after_m2"))
         weigh(2)
         score(3, ("score0", "score1"), keep.tile([P, PACK, 2 * P], F32, name="probs3", align_bytes=64))
         quantize_h(1)
@@ -338,5 +338,5 @@ def tile_attend_gsig_x_ts_kernel(tc, xT, wT, y, wt, ts, offs, out):
         scale(TILES - 1, P // 2, P // 2)
         quantize_h(TILES - 1)
         product(TILES - 1)
-        store(TILES - 2, nc.scalar.copy, 1)
-        store(TILES - 1, nc.scalar.copy, 2)
+        store(TILES - 2, nc.scalar.copy, 2)
+        store(TILES - 1, nc.vector.tensor_copy, 2)

@@ -42,14 +42,14 @@ def tile_attend_gsig_x_ts_kernel(tc, xT, wT, y, wt, ts, offs, out):
         planes = [keep.tile([P, T], F32, name="plane%d" % t, tag="stage%d" % t, align_bytes=64) for t in range(PACK - 1)]
         ts_window = late.tile([P, T], F32, name="ts_window", align_bytes=64, offset=0)
         wt_runs = keep.tile([P, TILES], F32, name="wt_runs")
-        nc.vector.memset(ts_window[:, 0 : T // 2], 0.0)
-        nc.gpsimd.memset(ts_window[:, T // 2 : T], 0.0)
+        zero = keep.tile([P, 1], F32, name="zero")
+        nc.vector.memset(zero[:], 0.0)
+        nc.vector.memset(ts_window[:], 0.0)
         nc.sync.dma_start(planes[0][:, 0 : T // 2], w_rows[:, 0, 0 : T // 2])
         nc.sync.dma_start(wt_runs[:], wt[0].rearrange("(n m) o -> n (m o)", n=P))
         nc.sync.dma_start(offsets[:], offs)
-        nc.sync.dma_start(ts_window[0:1, 0 : T // 2], ts[0:1, 0 : T // 2])
-        nc.sync.dma_start(ts_window[0:1, T // 2 : T], ts[0:1, T // 2 : T])
         nc.sync.dma_start(planes[0][:, T // 2 : T], w_rows[:, 0, T // 2 : T])
+        nc.sync.dma_start(ts_window[0:1, :], ts[0:1, :])
         x_rows = xT[0].rearrange("(p t) r -> p t r", t=PACK)
         y_rows = y[0].rearrange("(k p) i -> p k i", p=P)
         x_raw, y_raw = {}, {}
@@ -75,7 +75,7 @@ def tile_attend_gsig_x_ts_kernel(tc, xT, wT, y, wt, ts, offs, out):
         ident_bf = keep.tile([P, P], BF16, name="ident_bf")
         make_identity(nc, ident_bf[:])
         warm = keep.tile([P, 1], F32, name="warm")
-        nc.scalar.activation(warm[:], ident[:, 0:1], SIGMOID)
+        nc.scalar.activation(warm[:], zero[:], SIGMOID)
 
         neg_wt = [
             keep.tile([P, HALF], F32, name="neg_wt0", tag="wt0", align_bytes=64),
@@ -93,7 +93,7 @@ def tile_attend_gsig_x_ts_kernel(tc, xT, wT, y, wt, ts, offs, out):
                 )
 
         ts_all = keep.tile([P, N], F32, name="ts_all")
-        nc.vector.tensor_copy(ts_all[:], ts_window[:].indirect(offsets[:]))
+        nc.scalar.activation(ts_all[:], ts_window[:].indirect(offsets[:]), COPY)
         planes.append(late.tile([P, T], F32, name="plane3", align_bytes=64, offset=0))
         nc.sync.dma_start(planes[PACK - 1][:], w_rows[:, PACK - 1, :])
         ts_col = []
@@ -251,8 +251,9 @@ def tile_attend_gsig_x_ts_kernel(tc, xT, wT, y, wt, ts, offs, out):
         first = keep.tile([P, 2 * N], F32, name="first", tag="stage1", align_bytes=64)
         load_x(0, 1, first[:, 0:N])
         load_y(0, 1, first[:, N : 2 * N])
+        for s in range(2, PACK):
+            nc.vector.tensor_scalar(factor[1][:, s, :], neg_wt[1][:], ts_col[s][:], None, MULT)
         gather(2)
-        make_factor(1, range(2, PACK))
         turn_plane(2, "grad0")
         second = keep.tile([P, 4 * N], F32, name="second", tag="stage2", align_bytes=64)
         load_x(1, 1, second[:, 0:N])

@@ -33,23 +33,28 @@ def tile_attend_gsig_x_ts_kernel(tc, xT, wT, y, wt, ts, offs, out):
         keep = ctx.enter_context(tc.tile_pool(name="keep", bufs=1))
         ring = ctx.enter_context(tc.tile_pool(name="ring", bufs=3))
         shared = ctx.enter_context(tc.tile_pool(name="shared", bufs=1))
+        early = ctx.enter_context(tc.tile_pool(name="early", bufs=1))
         late = ctx.enter_context(tc.tile_pool(name="late", bufs=1))
         held = ctx.enter_context(tc.tile_pool(name="held", bufs=1))
         psum = ctx.enter_context(tc.psum_pool(name="psum", bufs=1))
 
         offsets = keep.tile([P, N // 16], U16, name="offsets")
         w_rows = wT.rearrange("(p t) c -> p t c", t=PACK)
-        planes = [keep.tile([P, T], F32, name="plane%d" % t, tag="stage%d" % t, align_bytes=64) for t in range(PACK - 1)]
+        planes = [
+            keep.tile([P, T], F32, name="plane0", align_bytes=64),
+            early.tile([P, T], F32, name="plane1", align_bytes=64, offset=0),
+            keep.tile([P, T], F32, name="plane2", tag="stage2", align_bytes=64),
+        ]
         ts_window = late.tile([P, T], F32, name="ts_window", align_bytes=64, offset=0)
         wt_runs = keep.tile([P, TILES], F32, name="wt_runs")
-        zero = keep.tile([P, 1], F32, name="zero")
-        nc.vector.memset(zero[:], 0.0)
-        nc.vector.memset(ts_window[:], 0.0)
+        nc.vector.memset(ts_window[:, 0 : T // 2], 0.0)
+        nc.gpsimd.memset(ts_window[:, T // 2 : T], 0.0)
         nc.sync.dma_start(planes[0][:, 0 : T // 2], w_rows[:, 0, 0 : T // 2])
         nc.sync.dma_start(wt_runs[:], wt[0].rearrange("(n m) o -> n (m o)", n=P))
         nc.sync.dma_start(offsets[:], offs)
+        nc.sync.dma_start(ts_window[0:1, 0 : T // 2], ts[0:1, 0 : T // 2])
+        nc.sync.dma_start(ts_window[0:1, T // 2 : T], ts[0:1, T // 2 : T])
         nc.sync.dma_start(planes[0][:, T // 2 : T], w_rows[:, 0, T // 2 : T])
-        nc.sync.dma_start(ts_window[0:1, :], ts[0:1, :])
         x_rows = xT[0].rearrange("(p t) r -> p t r", t=PACK)
         y_rows = y[0].rearrange("(k p) i -> p k i", p=P)
         x_raw, y_raw = {}, {}
@@ -75,7 +80,7 @@ def tile_attend_gsig_x_ts_kernel(tc, xT, wT, y, wt, ts, offs, out):
         ident_bf = keep.tile([P, P], BF16, name="ident_bf")
         make_identity(nc, ident_bf[:])
         warm = keep.tile([P, 1], F32, name="warm")
-        nc.scalar.activation(warm[:], zero[:], SIGMOID)
+        nc.scalar.activation(warm[:], ident[:, 0:1], SIGMOID)
 
         neg_wt = [
             keep.tile([P, HALF], F32, name="neg_wt0", tag="wt0", align_bytes=64),
@@ -93,7 +98,7 @@ def tile_attend_gsig_x_ts_kernel(tc, xT, wT, y, wt, ts, offs, out):
                 )
 
         ts_all = keep.tile([P, N], F32, name="ts_all")
-        nc.scalar.activation(ts_all[:], ts_window[:].indirect(offsets[:]), COPY)
+        nc.vector.tensor_copy(ts_all[:], ts_window[:].indirect(offsets[:]))
         planes.append(late.tile([P, T], F32, name="plane3", align_bytes=64, offset=0))
         nc.sync.dma_start(planes[PACK - 1][:], w_rows[:, PACK - 1, :])
         ts_col = []
@@ -122,22 +127,24 @@ def tile_attend_gsig_x_ts_kernel(tc, xT, wT, y, wt, ts, offs, out):
             for s in range(PACK):
                 nc.tensor.transpose(w_turned[:, s, :], w_words[:, s, :, 0], ident[:])
             halves = w_turned[:].rearrange("q s p -> q (s p)").bitcast(BF16)
-            w_by_slot[0] = keep.tile([P, 2, P, PACK], BF16, name="w_by_slot", tag="wt0", align_bytes=64)
-            nc.scalar.copy(w_by_slot[0][:], halves.rearrange("q (s p e) -> q e p s", s=PACK, e=2))
+            w_by_slot[0] = keep.tile([P, 2, 2, P // 2, PACK], BF16, name="w_by_slot", tag="wt0", align_bytes=64)
+            nc.scalar.copy(w_by_slot[0][:], halves.rearrange("q (s h p e) -> q h e p s", s=PACK, h=2, e=2))
 
         def turn_plane(t, bank):
             w_turned = psum.tile([P, PACK, P], BF16, name="plane_turned", tag=bank)
             for s in range(PACK):
                 nc.tensor.transpose(w_turned[:, s, :], w_by_d[:, s, :, t], ident_bf[:])
             if t == 2:
-                w_by_slot[1] = held.tile([P, 2, P, PACK], BF16, name="w_by_slot1", align_bytes=64, offset=2 * KIB)
-            nc.scalar.copy(w_by_slot[1][:, t - 2, :, :], w_turned[:].rearrange("q s p -> q p s"))
+                w_by_slot[1] = early.tile([P, 2, 2, P // 2, PACK], BF16, name="w_by_slot1", align_bytes=64, offset=0)
+            nc.scalar.copy(w_by_slot[1][:, :, t - 2, :, :], w_turned[:].rearrange("q s (h p) -> q h p s", h=2))
 
         def quantize_w2(u):
-            cols = slice(u * D // 2, (u + 1) * D // 2)
-            nc.vector.quantize_mx(
-                w2_codes[:, cols].bitcast(E4M3), w2_scales[:, cols], w_by_slot[u][:].rearrange("q e p s -> q (e p s)")
-            )
+            for h in range(2):
+                cols = slice((2 * h + u) * P, (2 * h + u + 1) * P)
+                nc.vector.quantize_mx(
+                    w2_codes[:, cols].bitcast(E4M3), w2_scales[:, cols],
+                    w_by_slot[u][:, h, :, :, :].rearrange("q e p s -> q (e p s)"),
+                )
 
         def quantize_w1(half):
             cols = slice(half * N // 2, (half + 1) * N // 2)
@@ -230,14 +237,25 @@ def tile_attend_gsig_x_ts_kernel(tc, xT, wT, y, wt, ts, offs, out):
 
         def store(k, copy, pieces):
             result = ring.tile([P, D], F32, name="result", bufs=4)
-            ordered = grads[k][:].rearrange("r (t p) -> r p t", t=PACK)
+            ordered = grads[k][:].rearrange("r (h t p) -> r h p t", h=2, t=PACK)
             for piece in range(pieces):
+                halves = slice(piece * 2 // pieces, (piece + 1) * 2 // pieces)
                 cols = slice(piece * D // pieces, (piece + 1) * D // pieces)
-                copy(
-                    result[:, cols].rearrange("r (p t) -> r p t", t=PACK),
-                    ordered[:, piece * P // pieces : (piece + 1) * P // pieces, :],
-                )
+                copy(result[:, cols].rearrange("r (h p t) -> r h p t", p=P // 2, t=PACK), ordered[:, halves, :, :])
                 nc.sync.dma_start(out[0, k * P : (k + 1) * P, cols], result[:, cols])
+
+        def finish_in_halves(k, banks, copies):
+            h_codes, h_scales = h_mx[k]
+            for h in range(2):
+                cols = slice(h * D // 2, (h + 1) * D // 2)
+                grad = psum.tile([P, D // 2], F32, name="grad_half", tag=banks[h])
+                nc.tensor.matmul_mx(
+                    grad[:], h_codes[:].bitcast(E5M2), h_scales[:], w2_codes[:, cols].bitcast(E4M3), w2_scales[:, cols],
+                    start=True, stop=True,
+                )
+                result = keep.tile([P, D // 2], F32, name="result_half%d" % h)
+                copies[h](result[:].rearrange("r (p t) -> r p t", t=PACK), grad[:].rearrange("r (t p) -> r p t", t=PACK))
+                nc.sync.dma_start(out[0, k * P : (k + 1) * P, cols], result[:])
 
         def gather(t):
             nc.vector.tensor_copy(w_by_d[:, :, :, t].rearrange("p s q -> p q s"), planes[t][:].indirect(offsets[:]))
@@ -248,13 +266,10 @@ def tile_attend_gsig_x_ts_kernel(tc, xT, wT, y, wt, ts, offs, out):
         make_factor(0, range(PACK))
         gather(1)
         turn_words("score0")
-        first = keep.tile([P, 2 * N], F32, name="first", tag="stage1", align_bytes=64)
-        load_x(0, 1, first[:, 0:N])
-        load_y(0, 1, first[:, N : 2 * N])
-        for s in range(2, PACK):
-            nc.vector.tensor_scalar(factor[1][:, s, :], neg_wt[1][:], ts_col[s][:], None, MULT)
+        load_x(0, 1, early.tile([P, N], F32, name="x_raw0", align_bytes=64, offset=0)[:])
+        load_y(0, 1, early.tile([P, N], F32, name="y_raw0", align_bytes=64, offset=2 * KIB)[:])
         gather(2)
-        turn_plane(2, "grad0")
+        make_factor(1, range(2, PACK))
         second = keep.tile([P, 4 * N], F32, name="second", tag="stage2", align_bytes=64)
         load_x(1, 1, second[:, 0:N])
         load_x(2, 2, second[:, N : 3 * N])
@@ -281,6 +296,7 @@ def tile_attend_gsig_x_ts_kernel(tc, xT, wT, y, wt, ts, offs, out):
             0, late.tile([P, P], U32, name="first_codes", align_bytes=64, offset=0),
             keep.tile([P, P], U8, name="first_scales", tag="after_m0", align_bytes=64),
         )
+        turn_plane(2, "grad2")
         quantize_w1(0)
         quantize_w1(1)
         cast_x(1, nc.scalar.copy, bf_tile(keep, P, "x_bf1"))
@@ -304,7 +320,7 @@ def tile_attend_gsig_x_ts_kernel(tc, xT, wT, y, wt, ts, offs, out):
         product(0)
         turn_y(3)
         scale(1, 0, P)
-        quantize_x(3, held.tile([P, 2 * P], U32, name="codes3", align_bytes=64, offset=2 * KIB), scales_tile(2 * P))
+        quantize_x(3, early.tile([P, 2 * P], U32, name="codes3", align_bytes=64, offset=0), scales_tile(2 * P))
         cast_x(4, nc.scalar.copy, bf_tile(keep, 2 * P, "x_bf4", tag="after_m2"))
         weigh(2)
         score(3, ("score0", "score1"), keep.tile([P, PACK, 2 * P], F32, name="probs3", align_bytes=64))
@@ -316,7 +332,7 @@ def tile_attend_gsig_x_ts_kernel(tc, xT, wT, y, wt, ts, offs, out):
         quantize_h(2)
         product(2)
         quantize_x(4, keep.tile([P, 2 * P], U32, name="codes4", align_bytes=64), scales_tile(2 * P))
-        deal_y(5, nc.scalar.copy, held.tile([P, PACK, P], F32, name="dealt5", align_bytes=64, offset=KIB // 2)[:])
+        deal_y(5, nc.scalar.copy, early.tile([P, PACK, P], F32, name="dealt5", align_bytes=64, offset=0)[:])
         turn_y(5)
         scale(3, 0, P)
         store(0, nc.scalar.copy, 1)
@@ -338,6 +354,5 @@ def tile_attend_gsig_x_ts_kernel(tc, xT, wT, y, wt, ts, offs, out):
         product(TILES - 2)
         scale(TILES - 1, P // 2, P // 2)
         quantize_h(TILES - 1)
-        product(TILES - 1)
         store(TILES - 2, nc.scalar.copy, 2)
-        store(TILES - 1, nc.vector.tensor_copy, 2)
+        finish_in_halves(TILES - 1, ("grad3", "score0"), (nc.scalar.copy, nc.vector.tensor_copy))

@@ -14,10 +14,9 @@ U8 = mybir.dt.uint8
 E4M3 = mybir.dt.float8_e4m3fn_x4
 E5M2 = mybir.dt.float8_e5m2_x4
 MULT = mybir.AluOpType.mult
-MAX = mybir.AluOpType.max
 SUB = mybir.AluOpType.subtract
 COPY = mybir.ActivationFunctionType.Copy
-SIGMOID = mybir.ActivationFunctionType.Sigmoid
+TANH = mybir.ActivationFunctionType.Tanh
 
 P = 128
 PACK = 4
@@ -80,7 +79,7 @@ def tile_attend_gsig_x_ts_kernel(tc, xT, wT, y, wt, ts, offs, out):
         ident_bf = keep.tile([P, P], BF16, name="ident_bf")
         make_identity(nc, ident_bf[:])
         warm = keep.tile([P, 1], F32, name="warm")
-        nc.scalar.activation(warm[:], ident[:, 0:1], SIGMOID)
+        nc.scalar.activation(warm[:], ident[:, 0:1], TANH)
 
         neg_wt = [
             keep.tile([P, HALF], F32, name="neg_wt0", tag="wt0", align_bytes=64),
@@ -106,7 +105,7 @@ def tile_attend_gsig_x_ts_kernel(tc, xT, wT, y, wt, ts, offs, out):
             ts_turned = psum.tile([P, P], F32, name="ts_turned", tag=("grad0", "grad1", "grad2", "score1")[s])
             nc.tensor.transpose(ts_turned[:], ts_all[:, s::PACK], ident[:])
             ts_col.append(keep.tile([P, 1], F32, name="ts_col%d" % s))
-            nc.scalar.copy(ts_col[s][:], ts_turned[:, 0:1])
+            nc.scalar.activation(ts_col[s][:], ts_turned[:, 0:1], COPY, scale=0.5)
 
         factor = [keep.tile([P, PACK, HALF], F32, name="factor%d" % h) for h in range(2)]
 
@@ -189,7 +188,7 @@ def tile_attend_gsig_x_ts_kernel(tc, xT, wT, y, wt, ts, offs, out):
                     )
                 for e in range(share):
                     s = share * b + e
-                    nc.scalar.activation(chunk[:, s, :], scores[:, e, :], SIGMOID, scale=ts_col[s][:])
+                    nc.scalar.activation(chunk[:, s, :], scores[:, e, :], TANH, scale=ts_col[s][:])
             for j, k in enumerate(CHUNKS[c]):
                 probs[k] = chunk[:, :, j * P : (j + 1) * P]
 
@@ -206,9 +205,31 @@ def tile_attend_gsig_x_ts_kernel(tc, xT, wT, y, wt, ts, offs, out):
                 column = columns[k][s] if k in columns else y_raw[k][:, s::PACK]
                 nc.tensor.transpose(labels[k][:, s, :], column, ident[:])
 
+        negated = {}
+
+        def negate_tanh(k, bank):
+            turned = psum.tile([P, PACK, P], F32, name="tanh_turned", tag=bank)
+            for s in range(PACK):
+                nc.tensor.transpose(turned[:, s, :], probs[k][:, s, :], ident[:])
+            negated[k] = keep.tile([P, PACK, P], F32, name="negated%d" % k, align_bytes=64)
+            nc.scalar.activation(negated[k][:], turned[:], COPY, scale=-1.0)
+
+        def weigh_in_psum(k, bank):
+            diffs[k] = psum.tile([P, PACK, P], F32, name="labels", tag=bank)
+            for s in range(PACK):
+                column = columns[k][s] if k in columns else y_raw[k][:, s::PACK]
+                nc.tensor.matmul(diffs[k][:, s, :], column, ident[:], start=s == 0, stop=False, is_transpose=True)
+            for s in range(PACK):
+                nc.tensor.matmul(
+                    diffs[k][:, s, :], negated[k][:, s, :], ident[:], start=False, stop=s == PACK - 1, is_transpose=True
+                )
+
         def weigh(k):
-            diffs[k] = ring.tile([P, PACK, P], F32, name="diff", bufs=3)
-            nc.vector.scalar_tensor_tensor(diffs[k][:], labels[k][:], 0.0, probs[k], MAX, SUB)
+            if k == 3:
+                diffs[k] = keep.tile([P, PACK, P], F32, name="diff3", tag="after_m2", align_bytes=64)
+            else:
+                diffs[k] = ring.tile([P, PACK, P], F32, name="diff", bufs=3)
+            nc.vector.tensor_tensor(diffs[k][:], labels[k][:], probs[k], SUB)
 
         def scale(k, first, count):
             rows = slice(k % 4 * P + first, k % 4 * P + first + count)
@@ -222,8 +243,8 @@ def tile_attend_gsig_x_ts_kernel(tc, xT, wT, y, wt, ts, offs, out):
             )
 
         def quantize_h(k):
-            h_codes = ring.tile([P, P], U32, name="h_codes", align_bytes=64)
-            h_scales = ring.tile([P, P], U8, name="h_scales", align_bytes=64)
+            h_codes = ring.tile([P, P], U32, name="h_codes", align_bytes=64, bufs=TILES)
+            h_scales = ring.tile([P, P], U8, name="h_scales", align_bytes=64, bufs=TILES)
             nc.vector.quantize_mx(h_codes[:].bitcast(E5M2), h_scales[:], h_bf[k][:].rearrange("q r s -> q (r s)"))
             h_mx[k] = (h_codes, h_scales)
 
@@ -236,7 +257,7 @@ def tile_attend_gsig_x_ts_kernel(tc, xT, wT, y, wt, ts, offs, out):
             )
 
         def store(k, copy, pieces):
-            result = ring.tile([P, D], F32, name="result", bufs=4)
+            result = ring.tile([P, D], F32, name="result", bufs=TILES - 1)
             ordered = grads[k][:].rearrange("r (h t p) -> r h p t", h=2, t=PACK)
             for piece in range(pieces):
                 halves = slice(piece * 2 // pieces, (piece + 1) * 2 // pieces)
@@ -328,31 +349,39 @@ def tile_attend_gsig_x_ts_kernel(tc, xT, wT, y, wt, ts, offs, out):
         turn_y(4)
         product(1)
         scale(2, 0, P)
-        weigh(3)
+        quantize_x(4, keep.tile([P, 2 * P], U32, name="codes4", align_bytes=64), scales_tile(2 * P))
         quantize_h(2)
         product(2)
-        quantize_x(4, keep.tile([P, 2 * P], U32, name="codes4", align_bytes=64), scales_tile(2 * P))
-        deal_y(5, nc.scalar.copy, early.tile([P, PACK, P], F32, name="dealt5", align_bytes=64, offset=0)[:])
+        weigh(3)
         turn_y(5)
-        scale(3, 0, P)
         store(0, nc.scalar.copy, 1)
+        scale(3, 0, P)
         score(4, ("score0", "score1"), keep.tile([P, PACK, 2 * P], F32, name="probs4", align_bytes=64))
         store(1, nc.scalar.copy, 1)
+        negate_tanh(7, "score1")
         store(2, nc.scalar.copy, 1)
-        for k in (4, 5, 6):
-            weigh(k)
-            quantize_h(k - 1)
-            if k + 2 < TILES:
-                turn_y(k + 2)
-            product(k - 1)
-            store(k - 1, nc.scalar.copy, 1)
-            if k == 6:
-                weigh(7)
-            scale(k, 0, P)
-        scale(TILES - 1, 0, P // 2)
-        quantize_h(TILES - 2)
-        product(TILES - 2)
-        scale(TILES - 1, P // 2, P // 2)
-        quantize_h(TILES - 1)
-        store(TILES - 2, nc.scalar.copy, 2)
-        finish_in_halves(TILES - 1, ("grad3", "score0"), (nc.scalar.copy, nc.vector.tensor_copy))
+        weigh(4)
+        quantize_h(3)
+        turn_y(6)
+        product(3)
+        store(3, nc.scalar.copy, 1)
+        scale(4, 0, P)
+        weigh(5)
+        quantize_h(4)
+        product(4)
+        weigh_in_psum(7, "score0")
+        store(4, nc.scalar.copy, 1)
+        weigh(6)
+        scale(5, 0, P)
+        scale(6, 0, P // 2)
+        quantize_h(5)
+        product(5)
+        store(5, nc.scalar.copy, 1)
+        scale(6, P // 2, P // 2)
+        scale(7, 0, P // 2)
+        quantize_h(6)
+        product(6)
+        scale(7, P // 2, P // 2)
+        quantize_h(7)
+        store(6, nc.scalar.copy, 2)
+        finish_in_halves(7, ("grad3", "label1"), (nc.vector.tensor_copy, nc.scalar.copy))

@@ -78,8 +78,6 @@ def tile_attend_gsig_x_ts_kernel(tc, xT, wT, y, wt, ts, offs, out):
         make_identity(nc, ident[:])
         ident_bf = keep.tile([P, P], BF16, name="ident_bf")
         make_identity(nc, ident_bf[:])
-        warm = keep.tile([P, 1], F32, name="warm")
-        nc.scalar.activation(warm[:], ident[:, 0:1], TANH)
 
         neg_wt = [
             keep.tile([P, HALF], F32, name="neg_wt0", tag="wt0", align_bytes=64),

@@ -197,8 +197,8 @@ def tile_attend_gsig_x_ts_kernel(tc, xT, wT, y, wt, ts, offs, out):
             )
             columns[k] = [dealt[:, s, :] for s in range(PACK)]
 
-        def turn_y(k):
-            labels[k] = psum.tile([P, PACK, P], F32, name="labels", tag="label%d" % (k % 2))
+        def turn_y(k, bank=None):
+            labels[k] = psum.tile([P, PACK, P], F32, name="labels", tag=bank or "label%d" % (k % 2))
             for s in range(PACK):
                 column = columns[k][s] if k in columns else y_raw[k][:, s::PACK]
                 nc.tensor.transpose(labels[k][:, s, :], column, ident[:])
@@ -330,7 +330,7 @@ def tile_attend_gsig_x_ts_kernel(tc, xT, wT, y, wt, ts, offs, out):
         cast_x(3, nc.scalar.copy, bf_tile(keep, P, "x_bf3a", tag="after_m1"))
         turn_plane(3, "label0")
         score(2, ("score0", "score1"), keep.tile([P, PACK, 2 * P], F32, name="probs2", tag="after_w3", align_bytes=64))
-        turn_y(2)
+        turn_y(2, "grad3")
         weigh(1)
         quantize_h(0)
         cast_x(3, nc.vector.tensor_copy, bf_tile(held, P, "x_bf3b", offset=6 * KIB), P)

from contextlib import ExitStack

import concourse.mybir as mybir
from concourse.masks import make_identity

N, T, D, R = 512, 2048, 512, 1024
FLOPS = 2 * 2 * R * N * D

F32 = mybir.dt.float32
BF16 = mybir.dt.bfloat16
U32 = mybir.dt.uint32
U16 = mybir.dt.uint16
U8 = mybir.dt.uint8
E4M3 = mybir.dt.float8_e4m3fn_x4
E5M2 = mybir.dt.float8_e5m2_x4
MULT = mybir.AluOpType.mult
SUB = mybir.AluOpType.subtract
COPY = mybir.ActivationFunctionType.Copy
TANH = mybir.ActivationFunctionType.Tanh

P = 128
PACK = 4
TILES = R // P
HALF = R // 2
CHUNKS = [(0,), (1,), (2, 3), (4, 5), (6, 7)]
KIB = 1024


def tile_attend_gsig_x_ts_kernel(tc, xT, wT, y, wt, ts, offs, out):
    nc = tc.nc
    with ExitStack() as ctx:
        keep = ctx.enter_context(tc.tile_pool(name="keep", bufs=1))
        ring = ctx.enter_context(tc.tile_pool(name="ring", bufs=3))
        shared = ctx.enter_context(tc.tile_pool(name="shared", bufs=1))
        early = ctx.enter_context(tc.tile_pool(name="early", bufs=1))
        late = ctx.enter_context(tc.tile_pool(name="late", bufs=1))
        held = ctx.enter_context(tc.tile_pool(name="held", bufs=1))
        psum = ctx.enter_context(tc.psum_pool(name="psum", bufs=1))

        offsets = keep.tile([P, N // 16], U16, name="offsets")
        w_rows = wT.rearrange("(p t) c -> p t c", t=PACK)
        planes = [
            keep.tile([P, T], F32, name="plane0", align_bytes=64),
            early.tile([P, T], F32, name="plane1", align_bytes=64, offset=0),
            keep.tile([P, T], F32, name="plane2", tag="stage2", align_bytes=64),
        ]
        ts_window = late.tile([P, T], F32, name="ts_window", align_bytes=64, offset=0)
        wt_runs = keep.tile([P, TILES], F32, name="wt_runs")
        nc.vector.memset(ts_window[:, 0 : T // 2], 0.0)
        nc.gpsimd.memset(ts_window[:, T // 2 : T], 0.0)
        nc.sync.dma_start(planes[0][:, 0 : T // 2], w_rows[:, 0, 0 : T // 2])
        nc.sync.dma_start(wt_runs[:], wt[0].rearrange("(n m) o -> n (m o)", n=P))
        nc.sync.dma_start(offsets[:], offs)
        nc.sync.dma_start(ts_window[0:1, 0 : T // 2], ts[0:1, 0 : T // 2])
        nc.sync.dma_start(ts_window[0:1, T // 2 : T], ts[0:1, T // 2 : T])
        nc.sync.dma_start(planes[0][:, T // 2 : T], w_rows[:, 0, T // 2 : T])
        x_rows = xT[0].rearrange("(p t) r -> p t r", t=PACK)
        y_rows = y[0].rearrange("(k p) i -> p k i", p=P)
        x_raw, y_raw = {}, {}

        def load_x(k, count, stage):
            view = stage.rearrange("p (t r) -> p t r", t=PACK)
            nc.sync.dma_start(view, x_rows[:, :, k * P : (k + count) * P])
            for c, tiles in enumerate(CHUNKS):
                if k <= tiles[0] < k + count:
                    x_raw[c] = view[:, :, (tiles[0] - k) * P : (tiles[-1] + 1 - k) * P]

        def load_y(k, count, stage):
            view = stage.rearrange("p (j i) -> p j i", j=count)
            nc.sync.dma_start(view, y_rows[:, k : k + count, :])
            for j in range(count):
                y_raw[k + j] = view[:, j, :]

        for t in range(1, PACK - 1):
            nc.sync.dma_start(planes[t][:], w_rows[:, t, :])

        ident = keep.tile([P, P], F32, name="ident")
        make_identity(nc, ident[:])
        ident_bf = keep.tile([P, P], BF16, name="ident_bf")
        make_identity(nc, ident_bf[:])

        neg_wt = [
            keep.tile([P, HALF], F32, name="neg_wt0", tag="wt0", align_bytes=64),
            held.tile([P, HALF], F32, name="neg_wt1", align_bytes=64, offset=2 * KIB),
        ]
        for b in range(TILES // PACK):
            spread = psum.tile([P, PACK, P], F32, name="spread", tag=("label1", "grad3")[b])
            for m in range(PACK):
                column = b * PACK + m
                nc.tensor.transpose(spread[:, m, :], wt_runs[:, column : column + 1].to_broadcast([P, P]), ident[:])
            for h in range(2):
                nc.scalar.activation(
                    neg_wt[h][:].rearrange("p (n m) -> p n m", m=TILES)[:, :, b * PACK : (b + 1) * PACK],
                    spread[:, :, h * P // 2 : (h + 1) * P // 2].rearrange("p m n -> p n m"), COPY, scale=-1.0,
                )

        ts_all = keep.tile([P, N], F32, name="ts_all")
        nc.vector.tensor_copy(ts_all[:], ts_window[:].indirect(offsets[:]))
        planes.append(late.tile([P, T], F32, name="plane3", align_bytes=64, offset=0))
        nc.sync.dma_start(planes[PACK - 1][:], w_rows[:, PACK - 1, :])
        ts_col = []
        for s in range(PACK):
            ts_turned = psum.tile([P, P], F32, name="ts_turned", tag=("grad0", "grad1", "grad2", "score1")[s])
            nc.tensor.transpose(ts_turned[:], ts_all[:, s::PACK], ident[:])
            ts_col.append(keep.tile([P, 1], F32, name="ts_col%d" % s))
            nc.scalar.activation(ts_col[s][:], ts_turned[:, 0:1], COPY, scale=0.5)

        factor = [keep.tile([P, PACK, HALF], F32, name="factor%d" % h) for h in range(2)]

        w_by_d = keep.tile([P, PACK, P, PACK], BF16, name="w_by_d", align_bytes=64)
        w_words = w_by_d[:].rearrange("p s q t -> p (s q t)").bitcast(F32).rearrange("p (s q u) -> p s q u", s=PACK, u=2)

        def make_factor(h, places):
            for s in places:
                nc.scalar.activation(factor[h][:, s, :], neg_wt[h][:], COPY, scale=ts_col[s][:])

        w1_codes = keep.tile([P, N], U32, name="w1_codes", align_bytes=64)
        w2_codes = keep.tile([P, D], U32, name="w2_codes", align_bytes=64)
        w2_scales = keep.tile([P, D], U8, name="w2_scales", align_bytes=64)
        w_by_slot, w1_scales = {}, {}

        def turn_words(bank):
            w_turned = psum.tile([P, PACK, P], F32, name="w_turned", tag=bank)
            for s in range(PACK):
                nc.tensor.transpose(w_turned[:, s, :], w_words[:, s, :, 0], ident[:])
            halves = w_turned[:].rearrange("q s p -> q (s p)").bitcast(BF16)
            w_by_slot[0] = keep.tile([P, 2, 2, P // 2, PACK], BF16, name="w_by_slot", tag="wt0", align_bytes=64)
            nc.scalar.copy(w_by_slot[0][:], halves.rearrange("q (s h p e) -> q h e p s", s=PACK, h=2, e=2))

        def turn_plane(t, bank):
            w_turned = psum.tile([P, PACK, P], BF16, name="plane_turned", tag=bank)
            for s in range(PACK):
                nc.tensor.transpose(w_turned[:, s, :], w_by_d[:, s, :, t], ident_bf[:])
            if t == 2:
                w_by_slot[1] = early.tile([P, 2, 2, P // 2, PACK], BF16, name="w_by_slot1", align_bytes=64, offset=0)
            nc.scalar.copy(w_by_slot[1][:, :, t - 2, :, :], w_turned[:].rearrange("q s (h p) -> q h p s", h=2))

        def quantize_w2(u):
            for h in range(2):
                cols = slice((2 * h + u) * P, (2 * h + u + 1) * P)
                nc.vector.quantize_mx(
                    w2_codes[:, cols].bitcast(E4M3), w2_scales[:, cols],
                    w_by_slot[u][:, h, :, :, :].rearrange("q e p s -> q (e p s)"),
                )

        def quantize_w1(half):
            cols = slice(half * N // 2, (half + 1) * N // 2)
            w1_scales[half] = shared.tile([P, N // 2], U8, name="w1_scales%d" % half, align_bytes=64, offset=half * N // 2)
            nc.vector.quantize_mx(
                w1_codes[:, cols].bitcast(E4M3), w1_scales[half][:],
                w_by_d[:, 2 * half : 2 * half + 2, :, :].rearrange("p s q t -> p (s q t)"),
            )

        x_bf, x_mx, probs, columns, labels, diffs, h_bf, h_mx, grads = {}, {}, {}, {}, {}, {}, {}, {}, {}

        def cast_x(c, copy, tile, first=0):
            width = tile.shape[1]
            copy(
                tile[:].rearrange("p (c i) t -> p c t i", i=4),
                x_raw[c][:, :, first : first + width].rearrange("p t (c i) -> p c t i", i=4),
            )
            x_bf.setdefault(c, []).append(tile)

        def quantize_x(c, x_codes, x_scales):
            first = 0
            for tile in x_bf[c]:
                cols = slice(first, first + tile.shape[1])
                nc.vector.quantize_mx(
                    x_codes[:, cols].bitcast(E4M3), x_scales[:, cols], tile[:].rearrange("p r t -> p (r t)")
                )
                first = cols.stop
            x_mx[c] = (x_codes, x_scales)

        def score(c, banks, chunk):
            x_codes, x_scales = x_mx[c]
            width = len(CHUNKS[c]) * P
            share = PACK // len(banks)
            for b, bank in enumerate(banks):
                scores = psum.tile([P, share, width], F32, name="scores", tag=bank)
                for e in range(share):
                    s = share * b + e
                    nc.tensor.matmul_mx(
                        scores[:, e, :], w1_codes[:, s * P : (s + 1) * P].bitcast(E4M3),
                        w1_scales[s // 2][:, s % 2 * P : (s % 2 + 1) * P],
                        x_codes[:].bitcast(E4M3), x_scales[:], start=True, stop=True,
                    )
                for e in range(share):
                    s = share * b + e
                    nc.scalar.activation(chunk[:, s, :], scores[:, e, :], TANH, scale=ts_col[s][:])
            for j, k in enumerate(CHUNKS[c]):
                probs[k] = chunk[:, :, j * P : (j + 1) * P]

        def deal_y(k, copy, dealt):
            copy(
                dealt.rearrange("p s (c i) -> p c s i", i=4),
                y_raw[k].rearrange("p (c i s) -> p c s i", i=4, s=PACK),
            )
            columns[k] = [dealt[:, s, :] for s in range(PACK)]

        def turn_y(k, bank=None):
            labels[k] = psum.tile([P, PACK, P], F32, name="labels", tag=bank or "label%d" % (k % 2))
            for s in range(PACK):
                column = columns[k][s] if k in columns else y_raw[k][:, s::PACK]
                nc.tensor.transpose(labels[k][:, s, :], column, ident[:])

        negated = {}

        def negate_tanh(k, bank):
            turned = psum.tile([P, PACK, P], F32, name="tanh_turned", tag=bank)
            for s in range(PACK):
                nc.tensor.transpose(turned[:, s, :], probs[k][:, s, :], ident[:])
            negated[k] = keep.tile([P, PACK, P], F32, name="negated%d" % k, align_bytes=64)
            nc.scalar.activation(negated[k][:], turned[:], COPY, scale=-1.0)

        def weigh_in_psum(k, bank):
            diffs[k] = psum.tile([P, PACK, P], F32, name="labels", tag=bank)
            for s in range(PACK):
                column = columns[k][s] if k in columns else y_raw[k][:, s::PACK]
                nc.tensor.matmul(diffs[k][:, s, :], column, ident[:], start=s == 0, stop=False, is_transpose=True)
            for s in range(PACK):
                nc.tensor.matmul(
                    diffs[k][:, s, :], negated[k][:, s, :], ident[:], start=False, stop=s == PACK - 1, is_transpose=True
                )

        def weigh(k):
            if k == 3:
                diffs[k] = keep.tile([P, PACK, P], F32, name="diff3", tag="after_m2", align_bytes=64)
            else:
                diffs[k] = ring.tile([P, PACK, P], F32, name="diff", bufs=3)
            nc.vector.tensor_tensor(diffs[k][:], labels[k][:], probs[k], SUB)

        def scale(k, first, count):
            rows = slice(k % 4 * P + first, k % 4 * P + first + count)
            if first == 0:
                h_bf[k] = ring.tile([P, P, PACK], BF16, name="h_bf", align_bytes=64, bufs=3)
            nc.vector.tensor_tensor(
                h_bf[k][:, first : first + count, :].rearrange("q (c i) s -> q c s i", i=4),
                diffs[k][:, :, first : first + count].rearrange("q s (c i) -> q c s i", i=4),
                factor[k // 4][:, :, rows].rearrange("q s (c i) -> q c s i", i=4),
                MULT,
            )

        def quantize_h(k):
            h_codes = ring.tile([P, P], U32, name="h_codes", align_bytes=64, bufs=TILES)
            h_scales = ring.tile([P, P], U8, name="h_scales", align_bytes=64, bufs=TILES)
            nc.vector.quantize_mx(h_codes[:].bitcast(E5M2), h_scales[:], h_bf[k][:].rearrange("q r s -> q (r s)"))
            h_mx[k] = (h_codes, h_scales)

        def product(k):
            h_codes, h_scales = h_mx[k]
            grads[k] = psum.tile([P, D], F32, name="grad", tag="grad%d" % (k % 4))
            nc.tensor.matmul_mx(
                grads[k][:], h_codes[:].bitcast(E5M2), h_scales[:], w2_codes[:].bitcast(E4M3), w2_scales[:],
                start=True, stop=True,
            )

        def store(k, copy, pieces):
            result = ring.tile([P, D], F32, name="result", bufs=TILES - 1)
            ordered = grads[k][:].rearrange("r (h t p) -> r h p t", h=2, t=PACK)
            for piece in range(pieces):
                halves = slice(piece * 2 // pieces, (piece + 1) * 2 // pieces)
                cols = slice(piece * D // pieces, (piece + 1) * D // pieces)
                copy(result[:, cols].rearrange("r (h p t) -> r h p t", p=P // 2, t=PACK), ordered[:, halves, :, :])
                nc.sync.dma_start(out[0, k * P : (k + 1) * P, cols], result[:, cols])

        def finish_in_halves(k, banks, copies):
            h_codes, h_scales = h_mx[k]
            for h in range(2):
                cols = slice(h * D // 2, (h + 1) * D // 2)
                grad = psum.tile([P, D // 2], F32, name="grad_half", tag=banks[h])
                nc.tensor.matmul_mx(
                    grad[:], h_codes[:].bitcast(E5M2), h_scales[:], w2_codes[:, cols].bitcast(E4M3), w2_scales[:, cols],
                    start=True, stop=True,
                )
                result = keep.tile([P, D // 2], F32, name="result_half%d" % h)
                copies[h](result[:].rearrange("r (p t) -> r p t", t=PACK), grad[:].rearrange("r (t p) -> r p t", t=PACK))
                nc.sync.dma_start(out[0, k * P : (k + 1) * P, cols], result[:])

        def gather(t):
            nc.vector.tensor_copy(w_by_d[:, :, :, t].rearrange("p s q -> p q s"), planes[t][:].indirect(offsets[:]))

        gather(0)
        for s in range(2):
            nc.vector.tensor_scalar(factor[1][:, s, :], neg_wt[1][:], ts_col[s][:], None, MULT)
        make_factor(0, range(PACK))
        gather(1)
        turn_words("score0")
        load_x(0, 1, early.tile([P, N], F32, name="x_raw0", align_bytes=64, offset=0)[:])
        load_y(0, 1, early.tile([P, N], F32, name="y_raw0", align_bytes=64, offset=2 * KIB)[:])
        gather(2)
        make_factor(1, range(2, PACK))
        second = keep.tile([P, 4 * N], F32, name="second", tag="stage2", align_bytes=64)
        load_x(1, 1, second[:, 0:N])
        load_x(2, 2, second[:, N : 3 * N])
        load_y(1, 1, second[:, 3 * N : 4 * N])
        turn_y(0)
        quantize_w2(0)
        gather(3)
        rest = late.tile([P, 10 * N], F32, name="rest", align_bytes=64, offset=N)
        load_x(4, 2, rest[:, 0 : 2 * N])
        load_y(2, 1, rest[:, 2 * N : 3 * N])
        load_y(3, 1, rest[:, 3 * N : 4 * N])
        load_x(6, 2, rest[:, 4 * N : 6 * N])
        for k in range(4, TILES):
            load_y(k, 1, rest[:, (k + 2) * N : (k + 3) * N])

        def bf_tile(pool, rows, name, **place):
            return pool.tile([P, rows, PACK], BF16, name=name, align_bytes=64, **place)

        def scales_tile(rows):
            return ring.tile([P, rows], U8, name="x_scales", align_bytes=64)

        cast_x(0, nc.scalar.copy, bf_tile(shared, P, "x_first", offset=0))
        quantize_x(
            0, late.tile([P, P], U32, name="first_codes", align_bytes=64, offset=0),
            keep.tile([P, P], U8, name="first_scales", tag="after_m0", align_bytes=64),
        )
        turn_plane(2, "grad2")
        quantize_w1(0)
        quantize_w1(1)
        cast_x(1, nc.scalar.copy, bf_tile(keep, P, "x_bf1"))
        score(0, ("label1", "grad0"), keep.tile([P, PACK, P], F32, name="probs0", tag="after_w0", align_bytes=64))
        quantize_x(1, keep.tile([P, P], U32, name="codes1", tag="after_m1", align_bytes=64), scales_tile(P))
        cast_x(2, nc.vector.tensor_copy, bf_tile(keep, 2 * P, "x_bf2", tag="after_m0"))
        score(1, ("grad1",), held.tile([P, PACK, P], F32, name="probs1", align_bytes=64, offset=6 * KIB))
        turn_y(1)
        quantize_x(2, keep.tile([P, 2 * P], U32, name="codes2", tag="after_m2", align_bytes=64), scales_tile(2 * P))
        weigh(0)
        scale(0, 0, P)
        cast_x(3, nc.scalar.copy, bf_tile(keep, P, "x_bf3a", tag="after_m1"))
        turn_plane(3, "label0")
        score(2, ("score0", "score1"), keep.tile([P, PACK, 2 * P], F32, name="probs2", tag="after_w3", align_bytes=64))
        turn_y(2, "grad3")
        weigh(1)
        quantize_h(0)
        cast_x(3, nc.vector.tensor_copy, bf_tile(held, P, "x_bf3b", offset=6 * KIB), P)
        deal_y(3, nc.vector.tensor_copy, held.tile([P, PACK, P], F32, name="dealt3", align_bytes=64, offset=7 * KIB)[:])
        quantize_w2(1)
        product(0)
        turn_y(3)
        scale(1, 0, P)
        quantize_x(3, early.tile([P, 2 * P], U32, name="codes3", align_bytes=64, offset=0), scales_tile(2 * P))
        cast_x(4, nc.scalar.copy, bf_tile(keep, 2 * P, "x_bf4", tag="after_m2"))
        weigh(2)
        score(3, ("score0", "score1"), keep.tile([P, PACK, 2 * P], F32, name="probs3", align_bytes=64))
        quantize_h(1)
        turn_y(4)
        product(1)
        scale(2, 0, P)
        quantize_x(4, keep.tile([P, 2 * P], U32, name="codes4", align_bytes=64), scales_tile(2 * P))
        quantize_h(2)
        product(2)
        weigh(3)
        turn_y(5)
        store(0, nc.scalar.copy, 1)
        scale(3, 0, P)
        score(4, ("score0", "score1"), keep.tile([P, PACK, 2 * P], F32, name="probs4", align_bytes=64))
        store(1, nc.scalar.copy, 1)
        negate_tanh(7, "score1")
        store(2, nc.scalar.copy, 1)
        weigh(4)
        quantize_h(3)
        turn_y(6)
        product(3)
        store(3, nc.scalar.copy, 1)
        scale(4, 0, P)
        weigh(5)
        quantize_h(4)
        product(4)
        weigh_in_psum(7, "score0")
        store(4, nc.scalar.copy, 1)
        weigh(6)
        scale(5, 0, P)
        scale(6, 0, P // 2)
        quantize_h(5)
        product(5)
        store(5, nc.scalar.copy, 1)
        scale(6, P // 2, P // 2)
        scale(7, 0, P // 2)
        quantize_h(6)
        product(6)
        scale(7, P // 2, P // 2)
        quantize_h(7)
        store(6, nc.scalar.copy, 2)
        finish_in_halves(7, ("grad3", "label1"), (nc.vector.tensor_copy, nc.scalar.copy))
